import numpy as np
import ml_dtypes


def mxq(x, axis, fmt="e4m3"):
    dtype, down = {"e4m3": (ml_dtypes.float8_e4m3fn, 7), "e5m2": (ml_dtypes.float8_e5m2, 14)}[fmt]
    v = np.moveaxis(np.asarray(x, np.float32).astype(ml_dtypes.bfloat16).astype(np.float64), axis, -1)
    blocks = v.reshape(v.shape[:-1] + (-1, 32))
    amax = np.abs(blocks).max(-1, keepdims=True)
    byte = np.maximum(np.where(amax > 0, np.frexp(amax)[1] - 1 + 127, 0) - down, 1)
    scale = np.exp2(byte - 127.0)
    codes = (blocks / scale).astype(np.float32).astype(dtype).astype(np.float64)
    return np.moveaxis((codes * scale).reshape(v.shape), -1, axis)


WIDE = False


def mx_kscale(k):
    if not WIDE:
        return np.ones(k)
    levels = np.array([10, -10, 5, -5, 0])
    if k % 512:
        return np.exp2(np.random.permutation(np.resize(levels, k // 32))).repeat(32)
    a = np.empty((k // 512, 16))
    for p in range(k // 512):
        a[p, :8] = np.random.permutation(np.resize(levels, 8))
        for g in range(8):
            far = levels[np.abs(levels - a[p, g]) >= 10]
            a[p, g + 8] = far[np.random.randint(len(far))]
    return np.exp2(a.ravel()).repeat(32)


def f64(x):
    return np.asarray(x).astype(np.float64)


def striped(idx):
    return np.tile(idx.reshape(-1, 16).T, (8, 1)).astype(np.uint16)


def unstriped(offs):
    return offs[:16].T.reshape(-1).astype(np.int64)


def pack_weight(w):
    k, n = w.shape
    w = f64(np.asarray(w, np.float32).astype(ml_dtypes.bfloat16)).reshape(k // 32, 32, n)
    amax = np.abs(w).max(1)
    byte = np.clip(np.where(amax > 0, np.frexp(amax)[1] - 1 + 127 - 7, 1), 1, 254)
    scaled = (w * np.exp2(127.0 - byte)[:, None, :]).reshape(k, n).astype(np.float32)
    words = np.ascontiguousarray(scaled.reshape(k // 512, 128, 4, n).transpose(0, 1, 3, 2)).astype(ml_dtypes.float8_e4m3fn).view(np.uint8)
    return words, np.ascontiguousarray(byte.astype(np.uint8).reshape(k // 512, 16, n))


def unpack_weight(words, scales):
    g, p, n, _ = words.shape
    vals = np.ascontiguousarray(words).view(ml_dtypes.float8_e4m3fn).astype(np.float64) * np.repeat(np.exp2(scales.astype(np.float64) - 127.0), 8, axis=1)[..., None]
    return vals.transpose(0, 1, 3, 2).reshape(g * 512, n)


def sigmoid(v):
    return 1.0 / (1.0 + np.exp(-np.maximum(v, -700.0)))

def planes(y):
    n, m = y.shape
    v = y.astype(np.float32).astype(ml_dtypes.bfloat16).astype(np.float64).reshape(n // 32, 32, m)
    top = np.abs(v).max(1)
    byte = np.clip(np.where(top > 0, np.frexp(top)[1] - 1 + 127 - 7, 1), 1, 254)
    codes = (v * np.exp2(127.0 - byte)[:, None, :]).reshape(n, m).astype(np.float32).astype(ml_dtypes.float8_e4m3fn).view(np.uint8)
    words = codes.reshape(n // 512, 128, 4, m).transpose(0, 1, 3, 2)
    return np.ascontiguousarray(words), np.ascontiguousarray(byte.astype(np.uint8).reshape(n // 512, 16, m))


K, T, N, U = 512, 512, 512, 1024


def setup_inputs():
    n = np.random.standard_normal
    s = mx_kscale(K)[:, None]
    packed_xT = pack_weight(n((K, T)) * s)
    return {
        "x_words": packed_xT[0],
        "x_scales": packed_xT[1],
        "mem": n((N, U)).astype(np.float32),
        "w1": (n((K, N)) / np.sqrt(K) / s).astype(np.float32),
        "slot": striped(np.random.permutation(U)[:T]),
    }


def reference(x_words, x_scales, mem, w1, slot):
    xq = unpack_weight(x_words, x_scales)
    y = mxq(f64(w1), 0, "e4m3").T @ xq
    out = f64(mem).copy()
    out[:, unstriped(slot)] = f64(mem)[:, unstriped(slot)] * sigmoid(y)
    return (out,) + planes(out)

@@ -1,0 +1,105 @@
+from contextlib import ExitStack
+
+import concourse.mybir as mybir
+
+F32 = mybir.dt.float32
+BF16 = mybir.dt.bfloat16
+I32 = mybir.dt.int32
+U32 = mybir.dt.uint32
+U16 = mybir.dt.uint16
+U8 = mybir.dt.uint8
+FP8X4 = mybir.dt.float8_e4m3fn_x4
+SIGMOID = mybir.ActivationFunctionType.Sigmoid
+MULT = mybir.AluOpType.mult
+
+P = 128
+PACK = 4
+K, T, N, U = 512, 512, 512, 1024
+PIECE = 512
+PIECES = U // PIECE
+SHARE = 256
+FLOPS = 2 * K * N * T
+
+
+def tile_picked_widxput_gate_lo_kernel(tc, x_words, x_scales, mem, w1, slot, out_0, out_1, out_2):
+    nc = tc.nc
+    with ExitStack() as ctx:
+        keep = ctx.enter_context(tc.tile_pool(name="keep", bufs=1))
+        psum = ctx.enter_context(tc.psum_pool(name="psum", bufs=1))
+
+        offsets = keep.tile([P, T // 16], U16, name="offsets")
+        x_codes = keep.tile([P, T], U32, name="x_codes", align_bytes=64)
+        x_plane = keep.tile([P, T], U8, name="x_plane", align_bytes=64)
+        w_raw = [keep.tile([P, PACK, N // 2], F32, name="w_raw%d" % h) for h in range(2)]
+        w_dealt = keep.tile([P, PACK * N], BF16, name="w_dealt", align_bytes=64)
+        w_codes = keep.tile([P, N], U32, name="w_codes", align_bytes=64)
+        w_plane = keep.tile([P, N], U8, name="w_plane", align_bytes=64)
+        store = [keep.tile([P, U], F32, name="store%d" % t, align_bytes=64) for t in range(PACK)]
+        old = [keep.tile([P, T], F32, name="old%d" % t, align_bytes=64) for t in range(PACK)]
+        gate = [keep.tile([P, T], F32, name="gate%d" % t, align_bytes=64) for t in range(PACK)]
+        woven = [keep.tile([P, PIECE, PACK], BF16, name="woven%d" % i, align_bytes=64) for i in range(PIECES)]
+        y_codes = keep.tile([P, U], U32, name="y_codes", align_bytes=64)
+        y_plane = keep.tile([P, U], U8, name="y_plane", align_bytes=64)
+        warm = keep.tile([P, 2], F32, name="warm")
+
+        mem_rows = mem.rearrange("(p t) c -> p t c", t=PACK)
+        out_rows = out_0.rearrange("(p t) c -> p t c", t=PACK)
+        w_rows = w1.rearrange("(p j) c -> p j c", j=PACK)
+
+        nc.vector.memset(warm[:, 0:1], 0.0)
+        nc.vector.memset(x_plane[:].bitcast(I32), 0)
+        nc.scalar.activation(warm[:, 1:2], warm[:, 0:1], SIGMOID)
+
+        for h in range(2):
+            nc.sync.dma_start(w_raw[h][:], w_rows[:, :, h * (N // 2) : (h + 1) * (N // 2)])
+        nc.sync.dma_start(offsets[:], slot)
+        for t in range(1):
+            nc.sync.dma_start(store[t][:], mem_rows[:, t, :])
+        x_in = x_words[0].rearrange("p c r -> p (c r)").bitcast(I32)
+        nc.sync.dma_start(x_codes[:, : T // 2].bitcast(I32), x_in[:, : T // 2])
+        nc.sync.dma_start(store[1][:], mem_rows[:, 1, :])
+        nc.sync.dma_start(x_codes[:, T // 2 :].bitcast(I32), x_in[:, T // 2 :])
+        for q in range(4):
+            nc.scalar.dma_start(x_plane[32 * q : 32 * q + 4, :].bitcast(I32), x_scales[0][4 * q : 4 * q + 4, :].bitcast(I32))
+        for t in range(2, PACK):
+            nc.sync.dma_start(store[t][:], mem_rows[:, t, :])
+
+        dealt = w_dealt[:].rearrange("p (t m j) -> p m t j", t=PACK, j=PACK)
+        for h in range(2):
+            nc.vector.tensor_copy(dealt[:, h * 64 : (h + 1) * 64], w_raw[h][:].rearrange("p j (m t) -> p m t j", t=PACK))
+        nc.vector.quantize_mx(out=w_codes[:].bitcast(FP8X4), scales=w_plane[:], in_=w_dealt[:])
+
+        for t in range(PACK):
+            cols = slice(t * P, (t + 1) * P)
+            width = T // 2 if t == 0 else T
+            for first in range(0, T, width):
+                part = slice(first, first + width)
+                acc = psum.tile([P, width], F32, name="acc")
+                nc.tensor.matmul_mx(out=acc[:], lhsT=w_codes[:, cols].bitcast(FP8X4), lhsT_scale=w_plane[:, cols],
+                                    rhs=x_codes[:, part].bitcast(FP8X4), rhs_scale=x_plane[:, part], start=True, stop=True)
+                nc.scalar.activation(gate[t][:, part], acc[:], SIGMOID)
+
+        for t in range(PACK):
+            nc.vector.tensor_copy(old[t][:], store[t][:].indirect(offsets[:]))
+        for t in range(PACK):
+            nc.vector.tensor_tensor(store[t][:].indirect(offsets[:]), old[t][:], gate[t][:], MULT)
+            nc.sync.dma_start(out_rows[:, t, :], store[t][:])
+            for first, last in ((0, SHARE), (SHARE, PIECE)) if t >= 2 else ((0, PIECE),):
+                for i in range(PIECES):
+                    src = store[t][:, i * PIECE + first : i * PIECE + last]
+                    if t == 3 and first == 0:
+                        nc.vector.tensor_copy(woven[i][:, first:last, t], src)
+                    elif t == 2 and first == 0:
+                        nc.scalar.copy(woven[i][:, first:last, 2:4], src.unsqueeze(2).to_broadcast([P, last - first, 2]))
+                    else:
+                        nc.scalar.copy(woven[i][:, first:last, t], src)
+
+        words = out_1[0].rearrange("p c r -> p (c r)").bitcast(I32)
+        for i in range(PIECES):
+            cols = slice(i * PIECE, (i + 1) * PIECE)
+            nc.vector.quantize_mx(out=y_codes[:, cols].bitcast(FP8X4), scales=y_plane[:, cols],
+                                  in_=woven[i][:].rearrange("p c t -> p (c t)"))
+            nc.sync.dma_start(words[:, cols], y_codes[:, cols].bitcast(I32))
+        for q in range(4):
+            queue = nc.scalar if q % 2 == 0 else nc.sync
+            queue.dma_start(out_2[0][4 * q : 4 * q + 4, :].bitcast(I32), y_plane[32 * q : 32 * q + 4, :].bitcast(I32))

@@ -15,9 +15,9 @@ MULT = mybir.AluOpType.mult
 P = 128
 PACK = 4
 K, T, N, U = 512, 512, 512, 1024
-PIECE = 512
-PIECES = U // PIECE
-SHARE = 256
+PIECES = ((0, 512), (512, 256), (768, 256))
+EARLY = 384
+W_SHARE = 96
 FLOPS = 2 * K * N * T
 
 
@@ -28,16 +28,15 @@ def tile_picked_widxput_gate_lo_kernel(tc, x_words, x_scales, mem, w1, slot, out
         psum = ctx.enter_context(tc.psum_pool(name="psum", bufs=1))
 
         offsets = keep.tile([P, T // 16], U16, name="offsets")
-        x_codes = keep.tile([P, T], U32, name="x_codes", align_bytes=64)
+        x_codes = keep.tile([P, T], U32, name="x_codes", tag="first_life0", align_bytes=64)
         x_plane = keep.tile([P, T], U8, name="x_plane", align_bytes=64)
-        w_raw = [keep.tile([P, PACK, N // 2], F32, name="w_raw%d" % h) for h in range(2)]
+        w_raw = [keep.tile([P, 2, N], F32, name="w_raw%d" % h) for h in range(2)]
         w_dealt = keep.tile([P, PACK * N], BF16, name="w_dealt", align_bytes=64)
-        w_codes = keep.tile([P, N], U32, name="w_codes", align_bytes=64)
-        w_plane = keep.tile([P, N], U8, name="w_plane", align_bytes=64)
+        w_codes = keep.tile([P, N], U32, name="w_codes", tag="first_life512", align_bytes=64)
+        w_plane = keep.tile([P, N], U8, name="w_plane", tag="first_life768", align_bytes=64)
         store = [keep.tile([P, U], F32, name="store%d" % t, align_bytes=64) for t in range(PACK)]
         old = [keep.tile([P, T], F32, name="old%d" % t, align_bytes=64) for t in range(PACK)]
         gate = [keep.tile([P, T], F32, name="gate%d" % t, align_bytes=64) for t in range(PACK)]
-        woven = [keep.tile([P, PIECE, PACK], BF16, name="woven%d" % i, align_bytes=64) for i in range(PIECES)]
         y_codes = keep.tile([P, U], U32, name="y_codes", align_bytes=64)
         y_plane = keep.tile([P, U], U8, name="y_plane", align_bytes=64)
         warm = keep.tile([P, 2], F32, name="warm")
@@ -51,14 +50,14 @@ def tile_picked_widxput_gate_lo_kernel(tc, x_words, x_scales, mem, w1, slot, out
         nc.scalar.activation(warm[:, 1:2], warm[:, 0:1], SIGMOID)
 
         for h in range(2):
-            nc.sync.dma_start(w_raw[h][:], w_rows[:, :, h * (N // 2) : (h + 1) * (N // 2)])
+            nc.sync.dma_start(w_raw[h][:], w_rows[:, 2 * h : 2 * h + 2, :])
         nc.sync.dma_start(offsets[:], slot)
         for t in range(1):
             nc.sync.dma_start(store[t][:], mem_rows[:, t, :])
         x_in = x_words[0].rearrange("p c r -> p (c r)").bitcast(I32)
-        nc.sync.dma_start(x_codes[:, : T // 2].bitcast(I32), x_in[:, : T // 2])
+        nc.sync.dma_start(x_codes[:, :EARLY].bitcast(I32), x_in[:, :EARLY])
         nc.sync.dma_start(store[1][:], mem_rows[:, 1, :])
-        nc.sync.dma_start(x_codes[:, T // 2 :].bitcast(I32), x_in[:, T // 2 :])
+        nc.sync.dma_start(x_codes[:, EARLY:].bitcast(I32), x_in[:, EARLY:])
         for q in range(4):
             nc.scalar.dma_start(x_plane[32 * q : 32 * q + 4, :].bitcast(I32), x_scales[0][4 * q : 4 * q + 4, :].bitcast(I32))
         for t in range(2, PACK):
@@ -66,40 +65,45 @@ def tile_picked_widxput_gate_lo_kernel(tc, x_words, x_scales, mem, w1, slot, out
 
         dealt = w_dealt[:].rearrange("p (t m j) -> p m t j", t=PACK, j=PACK)
         for h in range(2):
-            nc.vector.tensor_copy(dealt[:, h * 64 : (h + 1) * 64], w_raw[h][:].rearrange("p j (m t) -> p m t j", t=PACK))
+            raw = w_raw[h][:].rearrange("p j (m t) -> p m t j", t=PACK)
+            split = P if h == 0 else W_SHARE
+            nc.vector.tensor_copy(dealt[:, :split, :, 2 * h : 2 * h + 2], raw[:, :split])
+            if split < P:
+                nc.scalar.copy(dealt[:, split:, :, 2 * h : 2 * h + 2], raw[:, split:])
         nc.vector.quantize_mx(out=w_codes[:].bitcast(FP8X4), scales=w_plane[:], in_=w_dealt[:])
 
         for t in range(PACK):
             cols = slice(t * P, (t + 1) * P)
-            width = T // 2 if t == 0 else T
-            for first in range(0, T, width):
+            for first, width in ((0, 256), (256, 128), (EARLY, 128)) if t == 0 else ((0, T),):
                 part = slice(first, first + width)
-                acc = psum.tile([P, width], F32, name="acc")
+                acc = psum.tile([P, width], F32, name="acc", tag="acc%d" % (first + width))
                 nc.tensor.matmul_mx(out=acc[:], lhsT=w_codes[:, cols].bitcast(FP8X4), lhsT_scale=w_plane[:, cols],
                                     rhs=x_codes[:, part].bitcast(FP8X4), rhs_scale=x_plane[:, part], start=True, stop=True)
                 nc.scalar.activation(gate[t][:, part], acc[:], SIGMOID)
 
+        woven = [keep.tile([P, width, PACK], BF16, name="woven%d" % first, tag="first_life%d" % first, align_bytes=64) for first, width in PIECES]
         for t in range(PACK):
             nc.vector.tensor_copy(old[t][:], store[t][:].indirect(offsets[:]))
         for t in range(PACK):
             nc.vector.tensor_tensor(store[t][:].indirect(offsets[:]), old[t][:], gate[t][:], MULT)
             nc.sync.dma_start(out_rows[:, t, :], store[t][:])
-            for first, last in ((0, SHARE), (SHARE, PIECE)) if t >= 2 else ((0, PIECE),):
-                for i in range(PIECES):
-                    src = store[t][:, i * PIECE + first : i * PIECE + last]
-                    if t == 3 and first == 0:
-                        nc.vector.tensor_copy(woven[i][:, first:last, t], src)
-                    elif t == 2 and first == 0:
-                        nc.scalar.copy(woven[i][:, first:last, 2:4], src.unsqueeze(2).to_broadcast([P, last - first, 2]))
+            for half in range(2) if t >= 2 else range(1):
+                for tile, (first, width) in zip(woven, PIECES):
+                    count = width // 2 if t >= 2 else width
+                    part = slice(half * count, (half + 1) * count)
+                    src = store[t][:, first : first + width][:, part]
+                    if t == 3 and half == 0:
+                        nc.vector.tensor_copy(tile[:, part, t], src)
+                    elif t == 2 and half == 0:
+                        nc.scalar.copy(tile[:, part, 2:4], src.unsqueeze(2).to_broadcast([P, count, 2]))
                     else:
-                        nc.scalar.copy(woven[i][:, first:last, t], src)
+                        nc.scalar.copy(tile[:, part, t], src)
 
         words = out_1[0].rearrange("p c r -> p (c r)").bitcast(I32)
-        for i in range(PIECES):
-            cols = slice(i * PIECE, (i + 1) * PIECE)
+        for tile, (first, width) in zip(woven, PIECES):
+            cols = slice(first, first + width)
             nc.vector.quantize_mx(out=y_codes[:, cols].bitcast(FP8X4), scales=y_plane[:, cols],
-                                  in_=woven[i][:].rearrange("p c t -> p (c t)"))
+                                  in_=tile[:].rearrange("p c t -> p (c t)"))
             nc.sync.dma_start(words[:, cols], y_codes[:, cols].bitcast(I32))
         for q in range(4):
-            queue = nc.scalar if q % 2 == 0 else nc.sync
-            queue.dma_start(out_2[0][4 * q : 4 * q + 4, :].bitcast(I32), y_plane[32 * q : 32 * q + 4, :].bitcast(I32))
+            nc.scalar.dma_start(out_2[0][4 * q : 4 * q + 4, :].bitcast(I32), y_plane[32 * q : 32 * q + 4, :].bitcast(I32))

@@ -15,9 +15,11 @@ MULT = mybir.AluOpType.mult
 P = 128
 PACK = 4
 K, T, N, U = 512, 512, 512, 1024
+LANES = (0, 2, 3, 1)
 PIECES = ((0, 512), (512, 256), (768, 256))
+LAST_VECTOR = (320, 128, 128)
 EARLY = 384
-W_SHARE = 96
+W_SHARE = 32
 FLOPS = 2 * K * N * T
 
 
@@ -28,15 +30,15 @@ def tile_picked_widxput_gate_lo_kernel(tc, x_words, x_scales, mem, w1, slot, out
         psum = ctx.enter_context(tc.psum_pool(name="psum", bufs=1))
 
         offsets = keep.tile([P, T // 16], U16, name="offsets")
-        x_codes = keep.tile([P, T], U32, name="x_codes", tag="first_life0", align_bytes=64)
+        x_codes = keep.tile([P, T], U32, name="x_codes", align_bytes=64)
         x_plane = keep.tile([P, T], U8, name="x_plane", align_bytes=64)
-        w_raw = [keep.tile([P, 2, N], F32, name="w_raw%d" % h) for h in range(2)]
+        w_raw = [keep.tile([P, PACK, N // 2], F32, name="w_raw%d" % h) for h in range(2)]
         w_dealt = keep.tile([P, PACK * N], BF16, name="w_dealt", align_bytes=64)
-        w_codes = keep.tile([P, N], U32, name="w_codes", tag="first_life512", align_bytes=64)
-        w_plane = keep.tile([P, N], U8, name="w_plane", tag="first_life768", align_bytes=64)
+        w_codes = keep.tile([P, N], U32, name="w_codes", align_bytes=64)
+        w_plane = keep.tile([P, N], U8, name="w_plane", align_bytes=64)
         store = [keep.tile([P, U], F32, name="store%d" % t, align_bytes=64) for t in range(PACK)]
         old = [keep.tile([P, T], F32, name="old%d" % t, align_bytes=64) for t in range(PACK)]
-        gate = [keep.tile([P, T], F32, name="gate%d" % t, align_bytes=64) for t in range(PACK)]
+        woven = [keep.tile([P, width, PACK], BF16, name="woven%d" % first, align_bytes=64) for first, width in PIECES]
         y_codes = keep.tile([P, U], U32, name="y_codes", align_bytes=64)
         y_plane = keep.tile([P, U], U8, name="y_plane", align_bytes=64)
         warm = keep.tile([P, 2], F32, name="warm")
@@ -44,60 +46,69 @@ def tile_picked_widxput_gate_lo_kernel(tc, x_words, x_scales, mem, w1, slot, out
         mem_rows = mem.rearrange("(p t) c -> p t c", t=PACK)
         out_rows = out_0.rearrange("(p t) c -> p t c", t=PACK)
         w_rows = w1.rearrange("(p j) c -> p j c", j=PACK)
+        x_in = x_words[0].rearrange("p c r -> p (c r)").bitcast(I32)
 
         nc.vector.memset(warm[:, 0:1], 0.0)
         nc.vector.memset(x_plane[:].bitcast(I32), 0)
         nc.scalar.activation(warm[:, 1:2], warm[:, 0:1], SIGMOID)
 
-        for h in range(2):
-            nc.sync.dma_start(w_raw[h][:], w_rows[:, 2 * h : 2 * h + 2, :])
+        def load(step):
+            nc.sync.dma_start(store[step][:], mem_rows[:, LANES[step], :])
+
+        def look_up(step):
+            nc.vector.tensor_copy(old[step][:], store[step][:].indirect(offsets[:]))
+
+        load(0)
         nc.sync.dma_start(offsets[:], slot)
-        for t in range(1):
-            nc.sync.dma_start(store[t][:], mem_rows[:, t, :])
-        x_in = x_words[0].rearrange("p c r -> p (c r)").bitcast(I32)
-        nc.sync.dma_start(x_codes[:, :EARLY].bitcast(I32), x_in[:, :EARLY])
-        nc.sync.dma_start(store[1][:], mem_rows[:, 1, :])
-        nc.sync.dma_start(x_codes[:, EARLY:].bitcast(I32), x_in[:, EARLY:])
+        load(1)
         for q in range(4):
-            nc.scalar.dma_start(x_plane[32 * q : 32 * q + 4, :].bitcast(I32), x_scales[0][4 * q : 4 * q + 4, :].bitcast(I32))
-        for t in range(2, PACK):
-            nc.sync.dma_start(store[t][:], mem_rows[:, t, :])
-
-        dealt = w_dealt[:].rearrange("p (t m j) -> p m t j", t=PACK, j=PACK)
+            nc.sync.dma_start(x_plane[32 * q : 32 * q + 4, :].bitcast(I32), x_scales[0][4 * q : 4 * q + 4, :].bitcast(I32))
         for h in range(2):
-            raw = w_raw[h][:].rearrange("p j (m t) -> p m t j", t=PACK)
-            split = P if h == 0 else W_SHARE
-            nc.vector.tensor_copy(dealt[:, :split, :, 2 * h : 2 * h + 2], raw[:, :split])
-            if split < P:
-                nc.scalar.copy(dealt[:, split:, :, 2 * h : 2 * h + 2], raw[:, split:])
-        nc.vector.quantize_mx(out=w_codes[:].bitcast(FP8X4), scales=w_plane[:], in_=w_dealt[:])
+            nc.sync.dma_start(w_raw[h][:], w_rows[:, :, h * N // 2 : (h + 1) * N // 2])
+        nc.sync.dma_start(x_codes[:, :EARLY].bitcast(I32), x_in[:, :EARLY])
+        load(2)
+        nc.sync.dma_start(x_codes[:, EARLY:].bitcast(I32), x_in[:, EARLY:])
+        load(3)
+        look_up(0)
+        look_up(1)
 
-        for t in range(PACK):
-            cols = slice(t * P, (t + 1) * P)
-            for first, width in ((0, 256), (256, 128), (EARLY, 128)) if t == 0 else ((0, T),):
+        dealt = w_dealt[:].rearrange("p (s h m j) -> p h m s j", s=PACK, h=2, j=PACK)
+        raw = [w_raw[h][:].rearrange("p j (m t) -> p m t j", t=PACK) for h in range(2)]
+        nc.vector.tensor_copy(dealt[:, 0], raw[0])
+        nc.vector.tensor_copy(dealt[:, 1, :, 0:2], raw[1][:, :, 0:2])
+        nc.vector.tensor_copy(dealt[:, 1, :W_SHARE, 2:4], raw[1][:, :W_SHARE, 2:4])
+        nc.scalar.copy(dealt[:, 1, W_SHARE:, 2:4], raw[1][:, W_SHARE:, 2:4])
+        for h in range(2):
+            cols = slice(h * N // 2, (h + 1) * N // 2)
+            nc.vector.quantize_mx(out=w_codes[:, cols].bitcast(FP8X4), scales=w_plane[:, cols],
+                                  in_=w_dealt[:, h * 2 * N : (h + 1) * 2 * N])
+
+        def gate_of(step):
+            cols = slice(LANES[step] * P, (LANES[step] + 1) * P)
+            gate = keep.tile([P, T], F32, name="gate", tag="gate%d" % (step % 3), align_bytes=64)
+            for first, width in ((0, 256), (256, 128), (EARLY, 128)) if step == 0 else ((0, T),):
                 part = slice(first, first + width)
-                acc = psum.tile([P, width], F32, name="acc", tag="acc%d" % (first + width))
+                acc = psum.tile([P, width], F32, name="acc", tag="acc%d_%d" % (step, first))
                 nc.tensor.matmul_mx(out=acc[:], lhsT=w_codes[:, cols].bitcast(FP8X4), lhsT_scale=w_plane[:, cols],
                                     rhs=x_codes[:, part].bitcast(FP8X4), rhs_scale=x_plane[:, part], start=True, stop=True)
-                nc.scalar.activation(gate[t][:, part], acc[:], SIGMOID)
+                nc.scalar.activation(gate[:, part], acc[:], SIGMOID)
+            return gate
 
-        woven = [keep.tile([P, width, PACK], BF16, name="woven%d" % first, tag="first_life%d" % first, align_bytes=64) for first, width in PIECES]
-        for t in range(PACK):
-            nc.vector.tensor_copy(old[t][:], store[t][:].indirect(offsets[:]))
-        for t in range(PACK):
-            nc.vector.tensor_tensor(store[t][:].indirect(offsets[:]), old[t][:], gate[t][:], MULT)
-            nc.sync.dma_start(out_rows[:, t, :], store[t][:])
-            for half in range(2) if t >= 2 else range(1):
-                for tile, (first, width) in zip(woven, PIECES):
-                    count = width // 2 if t >= 2 else width
-                    part = slice(half * count, (half + 1) * count)
-                    src = store[t][:, first : first + width][:, part]
-                    if t == 3 and half == 0:
-                        nc.vector.tensor_copy(tile[:, part, t], src)
-                    elif t == 2 and half == 0:
-                        nc.scalar.copy(tile[:, part, 2:4], src.unsqueeze(2).to_broadcast([P, count, 2]))
-                    else:
-                        nc.scalar.copy(tile[:, part, t], src)
+        gates = [gate_of(step) for step in range(3)]
+        look_up(2)
+        for step, lane in enumerate(LANES):
+            nc.vector.tensor_tensor(store[step][:].indirect(offsets[:]), old[step][:], gates[step][:], MULT)
+            nc.sync.dma_start(out_rows[:, lane, :], store[step][:])
+            for tile, (first, width), share in zip(woven, PIECES, LAST_VECTOR):
+                src = store[step][:, first : first + width]
+                if step < 3:
+                    nc.scalar.copy(tile[:, :, lane], src)
+                else:
+                    nc.vector.tensor_copy(tile[:, :share, lane], src[:, :share])
+                    nc.scalar.copy(tile[:, share:, lane], src[:, share:])
+            if step == 0:
+                gates.append(gate_of(3))
+                look_up(3)
 
         words = out_1[0].rearrange("p c r -> p (c r)").bitcast(I32)
         for tile, (first, width) in zip(woven, PIECES):
@@ -106,4 +117,4 @@ def tile_picked_widxput_gate_lo_kernel(tc, x_words, x_scales, mem, w1, slot, out
                                   in_=tile[:].rearrange("p c t -> p (c t)"))
             nc.sync.dma_start(words[:, cols], y_codes[:, cols].bitcast(I32))
         for q in range(4):
-            nc.scalar.dma_start(out_2[0][4 * q : 4 * q + 4, :].bitcast(I32), y_plane[32 * q : 32 * q + 4, :].bitcast(I32))
+            (nc.sync if q == 0 else nc.scalar).dma_start(out_2[0][4 * q : 4 * q + 4, :].bitcast(I32), y_plane[32 * q : 32 * q + 4, :].bitcast(I32))

@@ -19,7 +19,7 @@ LANES = (0, 2, 3, 1)
 PIECES = ((0, 512), (512, 256), (768, 256))
 LAST_VECTOR = (320, 128, 128)
 EARLY = 384
-W_SHARE = 32
+W_LATE = 32
 FLOPS = 2 * K * N * T
 
 
@@ -32,7 +32,7 @@ def tile_picked_widxput_gate_lo_kernel(tc, x_words, x_scales, mem, w1, slot, out
         offsets = keep.tile([P, T // 16], U16, name="offsets")
         x_codes = keep.tile([P, T], U32, name="x_codes", align_bytes=64)
         x_plane = keep.tile([P, T], U8, name="x_plane", align_bytes=64)
-        w_raw = [keep.tile([P, PACK, N // 2], F32, name="w_raw%d" % h) for h in range(2)]
+        w_raw = [keep.tile([P, 2, N], F32, name="w_raw%d" % h) for h in range(2)]
         w_dealt = keep.tile([P, PACK * N], BF16, name="w_dealt", align_bytes=64)
         w_codes = keep.tile([P, N], U32, name="w_codes", align_bytes=64)
         w_plane = keep.tile([P, N], U8, name="w_plane", align_bytes=64)
@@ -58,26 +58,24 @@ def tile_picked_widxput_gate_lo_kernel(tc, x_words, x_scales, mem, w1, slot, out
         def look_up(step):
             nc.vector.tensor_copy(old[step][:], store[step][:].indirect(offsets[:]))
 
-        load(0)
-        nc.sync.dma_start(offsets[:], slot)
-        load(1)
-        for q in range(4):
-            nc.sync.dma_start(x_plane[32 * q : 32 * q + 4, :].bitcast(I32), x_scales[0][4 * q : 4 * q + 4, :].bitcast(I32))
         for h in range(2):
-            nc.sync.dma_start(w_raw[h][:], w_rows[:, :, h * N // 2 : (h + 1) * N // 2])
+            nc.sync.dma_start(w_raw[h][:], w_rows[:, 2 * h : 2 * h + 2, :])
+        nc.sync.dma_start(offsets[:], slot)
+        load(0)
         nc.sync.dma_start(x_codes[:, :EARLY].bitcast(I32), x_in[:, :EARLY])
-        load(2)
+        load(1)
         nc.sync.dma_start(x_codes[:, EARLY:].bitcast(I32), x_in[:, EARLY:])
+        for q in range(4):
+            nc.scalar.dma_start(x_plane[32 * q : 32 * q + 4, :].bitcast(I32), x_scales[0][4 * q : 4 * q + 4, :].bitcast(I32))
+        load(2)
         load(3)
-        look_up(0)
-        look_up(1)
 
-        dealt = w_dealt[:].rearrange("p (s h m j) -> p h m s j", s=PACK, h=2, j=PACK)
-        raw = [w_raw[h][:].rearrange("p j (m t) -> p m t j", t=PACK) for h in range(2)]
-        nc.vector.tensor_copy(dealt[:, 0], raw[0])
-        nc.vector.tensor_copy(dealt[:, 1, :, 0:2], raw[1][:, :, 0:2])
-        nc.vector.tensor_copy(dealt[:, 1, :W_SHARE, 2:4], raw[1][:, :W_SHARE, 2:4])
-        nc.scalar.copy(dealt[:, 1, W_SHARE:, 2:4], raw[1][:, W_SHARE:, 2:4])
+        dealt = w_dealt[:].rearrange("p (t m e j) -> p m t e j", t=PACK, e=2, j=PACK)
+        raw = [w_raw[h][:].rearrange("p j (m e t) -> p m t e j", e=2, t=PACK) for h in range(2)]
+        nc.vector.tensor_copy(dealt[:, :, :, :, 0:2], raw[0])
+        nc.vector.tensor_copy(dealt[:, :, 0:2, :, 2:4], raw[1][:, :, 0:2])
+        nc.vector.tensor_copy(dealt[:, :W_LATE, 2:4, :, 2:4], raw[1][:, :W_LATE, 2:4])
+        nc.scalar.copy(dealt[:, W_LATE:, 2:4, :, 2:4], raw[1][:, W_LATE:, 2:4])
         for h in range(2):
             cols = slice(h * N // 2, (h + 1) * N // 2)
             nc.vector.quantize_mx(out=w_codes[:, cols].bitcast(FP8X4), scales=w_plane[:, cols],
@@ -88,14 +86,17 @@ def tile_picked_widxput_gate_lo_kernel(tc, x_words, x_scales, mem, w1, slot, out
             gate = keep.tile([P, T], F32, name="gate", tag="gate%d" % (step % 3), align_bytes=64)
             for first, width in ((0, 256), (256, 128), (EARLY, 128)) if step == 0 else ((0, T),):
                 part = slice(first, first + width)
-                acc = psum.tile([P, width], F32, name="acc", tag="acc%d_%d" % (step, first))
+                acc = psum.tile([P, width], F32, name="acc", tag="acc%d" % (first + width))
                 nc.tensor.matmul_mx(out=acc[:], lhsT=w_codes[:, cols].bitcast(FP8X4), lhsT_scale=w_plane[:, cols],
                                     rhs=x_codes[:, part].bitcast(FP8X4), rhs_scale=x_plane[:, part], start=True, stop=True)
                 nc.scalar.activation(gate[:, part], acc[:], SIGMOID)
             return gate
 
         gates = [gate_of(step) for step in range(3)]
+        look_up(0)
+        look_up(1)
         look_up(2)
+        look_up(3)
         for step, lane in enumerate(LANES):
             nc.vector.tensor_tensor(store[step][:].indirect(offsets[:]), old[step][:], gates[step][:], MULT)
             nc.sync.dma_start(out_rows[:, lane, :], store[step][:])
@@ -108,7 +109,6 @@ def tile_picked_widxput_gate_lo_kernel(tc, x_words, x_scales, mem, w1, slot, out
                     nc.scalar.copy(tile[:, share:, lane], src[:, share:])
             if step == 0:
                 gates.append(gate_of(3))
-                look_up(3)
 
         words = out_1[0].rearrange("p c r -> p (c r)").bitcast(I32)
         for tile, (first, width) in zip(woven, PIECES):

@@ -1,6 +1,7 @@
 from contextlib import ExitStack
 
 import concourse.mybir as mybir
+from concourse.masks import make_identity
 
 F32 = mybir.dt.float32
 BF16 = mybir.dt.bfloat16
@@ -15,11 +16,11 @@ MULT = mybir.AluOpType.mult
 P = 128
 PACK = 4
 K, T, N, U = 512, 512, 512, 1024
-LANES = (0, 2, 3, 1)
+HALF = 256
+GROUPS = 4
 PIECES = ((0, 512), (512, 256), (768, 256))
-LAST_VECTOR = (320, 128, 128)
-EARLY = 384
-W_LATE = 32
+LAST_VECTOR = (256, 256, 0)
+LATE = 128
 FLOPS = 2 * K * N * T
 
 
@@ -30,85 +31,156 @@ def tile_picked_widxput_gate_lo_kernel(tc, x_words, x_scales, mem, w1, slot, out
         psum = ctx.enter_context(tc.psum_pool(name="psum", bufs=1))
 
         offsets = keep.tile([P, T // 16], U16, name="offsets")
-        x_codes = keep.tile([P, T], U32, name="x_codes", align_bytes=64)
+        x_codes = [keep.tile([P, HALF], U32, name="x_codes%d" % h, align_bytes=64) for h in range(2)]
         x_plane = keep.tile([P, T], U8, name="x_plane", align_bytes=64)
-        w_raw = [keep.tile([P, 2, N], F32, name="w_raw%d" % h) for h in range(2)]
-        w_dealt = keep.tile([P, PACK * N], BF16, name="w_dealt", align_bytes=64)
-        w_codes = keep.tile([P, N], U32, name="w_codes", align_bytes=64)
+        w_raw = [keep.tile([P, PACK, HALF], F32, name="w_raw", tag="w_raw%d" % h, align_bytes=64) for h in range(2)]
+        w_even = [keep.tile([P, PACK * P], BF16, name="w_even", tag="w_even%d" % h, align_bytes=64) for h in range(2)]
+        w_odd = [keep.tile([P, PACK * P], BF16, name="w_odd0", align_bytes=64)]
+        first_codes = keep.tile([P, P], U32, name="first_codes", tag="first_codes", align_bytes=64)
+        later_codes = keep.tile([P, N - P], U32, name="later_codes", align_bytes=64)
         w_plane = keep.tile([P, N], U8, name="w_plane", align_bytes=64)
-        store = [keep.tile([P, U], F32, name="store%d" % t, align_bytes=64) for t in range(PACK)]
-        old = [keep.tile([P, T], F32, name="old%d" % t, align_bytes=64) for t in range(PACK)]
+        store = [keep.tile([P, U], F32, name="store", tag="store%d" % s, align_bytes=64) for s in range(4)]
+        early_old = keep.tile([P, 2, T], F32, name="early_old", align_bytes=64)
+        old = [early_old[:, 0, :], early_old[:, 1, :]]
+        turned = [keep.tile([P, 2, 2, P], BF16, name="turned%d" % i, align_bytes=64) for i in range(GROUPS)]
         woven = [keep.tile([P, width, PACK], BF16, name="woven%d" % first, align_bytes=64) for first, width in PIECES]
         y_codes = keep.tile([P, U], U32, name="y_codes", align_bytes=64)
         y_plane = keep.tile([P, U], U8, name="y_plane", align_bytes=64)
+        ident = keep.tile([P, P], F32, name="ident", align_bytes=64)
         warm = keep.tile([P, 2], F32, name="warm")
 
+        mem_even = mem.rearrange("(h p two) c -> p h two c", h=2, two=2)
+        out_even = out_0.rearrange("(h p two) c -> p h two c", h=2, two=2)
         mem_rows = mem.rearrange("(p t) c -> p t c", t=PACK)
         out_rows = out_0.rearrange("(p t) c -> p t c", t=PACK)
+        mem_of = [mem_even[:, 0, 0, :], mem_even[:, 1, 0, :], mem_rows[:, 1, :], mem_rows[:, 3, :]]
+        out_of = [out_even[:, 0, 0, :], out_even[:, 1, 0, :], out_rows[:, 1, :], out_rows[:, 3, :]]
         w_rows = w1.rearrange("(p j) c -> p j c", j=PACK)
         x_in = x_words[0].rearrange("p c r -> p (c r)").bitcast(I32)
 
-        nc.vector.memset(warm[:, 0:1], 0.0)
         nc.vector.memset(x_plane[:].bitcast(I32), 0)
+        nc.vector.memset(warm[:, 0:1], 0.0)
         nc.scalar.activation(warm[:, 1:2], warm[:, 0:1], SIGMOID)
+        make_identity(nc, ident[:])
 
-        def load(step):
-            nc.sync.dma_start(store[step][:], mem_rows[:, LANES[step], :])
+        nc.sync.dma_start(w_raw[0][:], w_rows[:, :, :HALF])
+        for q in range(4):
+            nc.sync.dma_start(x_plane[32 * q : 32 * q + 4, :].bitcast(I32), x_scales[0][4 * q : 4 * q + 4, :].bitcast(I32))
+        nc.sync.dma_start(offsets[:], slot)
+        nc.sync.dma_start(store[0][:], mem_of[0])
+        nc.sync.dma_start(x_codes[0][:].bitcast(I32), x_in[:, :HALF])
+        nc.sync.dma_start(store[1][:], mem_of[1])
+        nc.sync.dma_start(w_raw[1][:], w_rows[:, :, HALF:])
+        nc.sync.dma_start(x_codes[1][:].bitcast(I32), x_in[:, HALF:])
+        for step in (2, 3):
+            nc.sync.dma_start(store[step][:], mem_of[step])
+
+        def cast_even(copy, h):
+            copy(w_even[h][:].rearrange("p (m j) -> p m j", j=PACK),
+                 w_raw[h][:].rearrange("p j (m two) -> p m j two", two=2)[:, :, :, 0])
+
+        def cast_odd(copy, h):
+            copy(w_odd[h][:].rearrange("p (u g j) -> p u g j", u=2, j=PACK),
+                 w_raw[h][:].rearrange("p j (g u two) -> p u g j two", u=2, two=2)[:, :, :, :, 1])
+
+        def codes(first, width):
+            tile, at = (first_codes, first) if first < P else (later_codes, first - P)
+            return tile[:, at : at + width].bitcast(FP8X4)
+
+        def quantise(src, first):
+            width = src.shape[1] // PACK
+            nc.vector.quantize_mx(out=codes(first, width), scales=w_plane[:, first : first + width], in_=src)
+
+        def quantise_odd(h):
+            for u in range(2):
+                quantise(w_odd[h][:, u * HALF : (u + 1) * HALF], (2 + u) * P + h * P // 2)
+
+        def gate_part(gate, step, first, width, bank):
+            cols = slice(step * P, (step + 1) * P)
+            acc = psum.tile([P, width], F32, name="acc", tag=bank)
+            for at in range(first, first + width, HALF):
+                wide = min(HALF, first + width - at)
+                nc.tensor.matmul_mx(out=acc[:, at - first : at - first + wide], lhsT=codes(step * P, P),
+                                    lhsT_scale=w_plane[:, cols],
+                                    rhs=x_codes[at // HALF][:, at % HALF : at % HALF + wide].bitcast(FP8X4),
+                                    rhs_scale=x_plane[:, at : at + wide], start=True, stop=True)
+            nc.scalar.activation(gate, acc[:], SIGMOID)
 
         def look_up(step):
-            nc.vector.tensor_copy(old[step][:], store[step][:].indirect(offsets[:]))
+            nc.vector.tensor_copy(old[step], store[step][:].indirect(offsets[:]))
 
-        for h in range(2):
-            nc.sync.dma_start(w_raw[h][:], w_rows[:, 2 * h : 2 * h + 2, :])
-        nc.sync.dma_start(offsets[:], slot)
-        load(0)
-        nc.sync.dma_start(x_codes[:, :EARLY].bitcast(I32), x_in[:, :EARLY])
-        load(1)
-        nc.sync.dma_start(x_codes[:, EARLY:].bitcast(I32), x_in[:, EARLY:])
-        for q in range(4):
-            nc.scalar.dma_start(x_plane[32 * q : 32 * q + 4, :].bitcast(I32), x_scales[0][4 * q : 4 * q + 4, :].bitcast(I32))
-        load(2)
-        load(3)
+        def put(step, gate, first, width):
+            part = slice(first, first + width)
+            nc.vector.tensor_tensor(store[step][:].indirect(offsets[:, first // 16 : (first + width) // 16]),
+                                    old[step][:, part], gate, MULT)
 
-        dealt = w_dealt[:].rearrange("p (t m e j) -> p m t e j", t=PACK, e=2, j=PACK)
-        raw = [w_raw[h][:].rearrange("p j (m e t) -> p m t e j", e=2, t=PACK) for h in range(2)]
-        nc.vector.tensor_copy(dealt[:, :, :, :, 0:2], raw[0])
-        nc.vector.tensor_copy(dealt[:, :, 0:2, :, 2:4], raw[1][:, :, 0:2])
-        nc.vector.tensor_copy(dealt[:, :W_LATE, 2:4, :, 2:4], raw[1][:, :W_LATE, 2:4])
-        nc.scalar.copy(dealt[:, W_LATE:, 2:4, :, 2:4], raw[1][:, W_LATE:, 2:4])
-        for h in range(2):
-            cols = slice(h * N // 2, (h + 1) * N // 2)
-            nc.vector.quantize_mx(out=w_codes[:, cols].bitcast(FP8X4), scales=w_plane[:, cols],
-                                  in_=w_dealt[:, h * 2 * N : (h + 1) * 2 * N])
+        def turn(h):
+            for i in range(GROUPS):
+                bank = psum.tile([P, 2, P], F32, name="bank", tag="turn%d" % i)
+                for u in range(2):
+                    block = 2 * i + u
+                    nc.tensor.transpose(bank[:, u, :], store[h][:, block * P : (block + 1) * P], ident[:])
+                nc.scalar.copy(turned[i][:, :, h, :], bank[:])
 
-        def gate_of(step):
-            cols = slice(LANES[step] * P, (LANES[step] + 1) * P)
-            gate = keep.tile([P, T], F32, name="gate", tag="gate%d" % (step % 3), align_bytes=64)
-            for first, width in ((0, 256), (256, 128), (EARLY, 128)) if step == 0 else ((0, T),):
-                part = slice(first, first + width)
-                acc = psum.tile([P, width], F32, name="acc", tag="acc%d" % (first + width))
-                nc.tensor.matmul_mx(out=acc[:], lhsT=w_codes[:, cols].bitcast(FP8X4), lhsT_scale=w_plane[:, cols],
-                                    rhs=x_codes[:, part].bitcast(FP8X4), rhs_scale=x_plane[:, part], start=True, stop=True)
-                nc.scalar.activation(gate[:, part], acc[:], SIGMOID)
-            return gate
+        def turn_back(i):
+            bank = psum.tile([P, 2, P], F32, name="bank", tag="turn%d" % i)
+            words_t = turned[i][:].rearrange("p u h r -> p (u h r)").bitcast(F32)
+            for u in range(2):
+                nc.tensor.transpose(bank[:, u, :], words_t[:, u * P : (u + 1) * P], ident[:])
+            tile = woven[max(0, i - 1)]
+            first = HALF if i == 1 else 0
+            pairs = bank[:].rearrange("p u c -> p (u c)").bitcast(BF16).rearrange("p (c e) -> p c e", e=2)
+            nc.scalar.copy(tile[:, first : first + HALF, 0:PACK:2], pairs)
 
-        gates = [gate_of(step) for step in range(3)]
+        first_gate = [keep.tile([P, HALF], F32, name="first_gate", tag="first_gate%d" % h, align_bytes=64) for h in range(2)]
+        second_gate = keep.tile([P, T], F32, name="second_gate", align_bytes=64)
+        last_gate = keep.tile([P, T], F32, name="last_gate", align_bytes=64)
+
+        cast_even(nc.vector.tensor_copy, 0)
+        cast_odd(nc.vector.tensor_copy, 0)
+        quantise(w_even[0][:], 0)
+        quantise_odd(0)
+        gate_part(first_gate[0][:], 0, 0, HALF, "acc0")
         look_up(0)
         look_up(1)
+        put(0, first_gate[0][:], 0, HALF)
+        cast_even(nc.scalar.copy, 1)
+        gate_part(first_gate[1][:], 0, HALF, HALF, "acc1")
+        w_odd.append(keep.tile([P, PACK * P], BF16, name="w_odd1", tag="first_codes", align_bytes=64))
+        cast_odd(nc.scalar.copy, 1)
+        quantise(w_even[1][:], P)
+        put(0, first_gate[1][:], HALF, HALF)
+        nc.sync.dma_start(out_of[0], store[0][:])
+        gate_part(second_gate[:], 1, 0, T, "acc1")
+        quantise_odd(1)
+        turn(0)
+        gate_part(last_gate[:, :HALF], 3, 0, HALF, "acc0")
+        gate_part(last_gate[:, HALF : T - LATE], 3, HALF, LATE, "acc2")
+        put(1, second_gate[:], 0, T)
+        nc.sync.dma_start(out_of[1], store[1][:])
+        third_gate = keep.tile([P, T], F32, name="third_gate", align_bytes=64)
+        gate_part(third_gate[:], 2, 0, T, "acc3")
+        late_old = keep.tile([P, 2, T], F32, name="late_old", tag="store0", align_bytes=64)
+        old.extend([late_old[:, 0, :], late_old[:, 1, :]])
         look_up(2)
         look_up(3)
-        for step, lane in enumerate(LANES):
-            nc.vector.tensor_tensor(store[step][:].indirect(offsets[:]), old[step][:], gates[step][:], MULT)
-            nc.sync.dma_start(out_rows[:, lane, :], store[step][:])
-            for tile, (first, width), share in zip(woven, PIECES, LAST_VECTOR):
-                src = store[step][:, first : first + width]
-                if step < 3:
-                    nc.scalar.copy(tile[:, :, lane], src)
-                else:
-                    nc.vector.tensor_copy(tile[:, :share, lane], src[:, :share])
-                    nc.scalar.copy(tile[:, share:, lane], src[:, share:])
-            if step == 0:
-                gates.append(gate_of(3))
+        turn(1)
+        for i in range(GROUPS):
+            turn_back(i)
+            if i == 2:
+                gate_part(last_gate[:, T - LATE :], 3, T - LATE, LATE, "turn0")
+        put(2, third_gate[:], 0, T)
+        nc.sync.dma_start(out_of[2], store[2][:])
+        for tile, (first, width) in zip(woven, PIECES):
+            nc.scalar.copy(tile[:, :, 1], store[2][:, first : first + width])
+        put(3, last_gate[:], 0, T)
+        nc.sync.dma_start(out_of[3], store[3][:])
+        for tile, (first, width), share in zip(woven, PIECES, LAST_VECTOR):
+            src = store[3][:, first : first + width]
+            if share:
+                nc.vector.tensor_copy(tile[:, :share, 3], src[:, :share])
+            if share < width:
+                nc.scalar.copy(tile[:, share:, 3], src[:, share:])
 
         words = out_1[0].rearrange("p c r -> p (c r)").bitcast(I32)
         for tile, (first, width) in zip(woven, PIECES):

@@ -19,7 +19,7 @@ K, T, N, U = 512, 512, 512, 1024
 HALF = 256
 GROUPS = 4
 PIECES = ((0, 512), (512, 256), (768, 256))
-LAST_VECTOR = (256, 256, 0)
+LAST_VECTOR = (288, 256, 0)
 LATE = 128
 FLOPS = 2 * K * N * T
 
@@ -31,7 +31,7 @@ def tile_picked_widxput_gate_lo_kernel(tc, x_words, x_scales, mem, w1, slot, out
         psum = ctx.enter_context(tc.psum_pool(name="psum", bufs=1))
 
         offsets = keep.tile([P, T // 16], U16, name="offsets")
-        x_codes = [keep.tile([P, HALF], U32, name="x_codes%d" % h, align_bytes=64) for h in range(2)]
+        x_codes = [keep.tile([P, HALF], U32, name="x_codes", tag="x_codes%d" % h, align_bytes=64) for h in range(2)]
         x_plane = keep.tile([P, T], U8, name="x_plane", align_bytes=64)
         w_raw = [keep.tile([P, PACK, HALF], F32, name="w_raw", tag="w_raw%d" % h, align_bytes=64) for h in range(2)]
         w_even = [keep.tile([P, PACK * P], BF16, name="w_even", tag="w_even%d" % h, align_bytes=64) for h in range(2)]
@@ -69,8 +69,8 @@ def tile_picked_widxput_gate_lo_kernel(tc, x_words, x_scales, mem, w1, slot, out
         nc.sync.dma_start(offsets[:], slot)
         nc.sync.dma_start(store[0][:], mem_of[0])
         nc.sync.dma_start(x_codes[0][:].bitcast(I32), x_in[:, :HALF])
-        nc.sync.dma_start(store[1][:], mem_of[1])
         nc.sync.dma_start(w_raw[1][:], w_rows[:, :, HALF:])
+        nc.sync.dma_start(store[1][:], mem_of[1])
         nc.sync.dma_start(x_codes[1][:].bitcast(I32), x_in[:, HALF:])
         for step in (2, 3):
             nc.sync.dma_start(store[step][:], mem_of[step])
@@ -159,8 +159,8 @@ def tile_picked_widxput_gate_lo_kernel(tc, x_words, x_scales, mem, w1, slot, out
         put(1, second_gate[:], 0, T)
         nc.sync.dma_start(out_of[1], store[1][:])
         third_gate = keep.tile([P, T], F32, name="third_gate", align_bytes=64)
-        gate_part(third_gate[:], 2, 0, T, "acc3")
-        late_old = keep.tile([P, 2, T], F32, name="late_old", tag="store0", align_bytes=64)
+        gate_part(third_gate[:], 2, 0, T, "acc1")
+        late_old = keep.tile([P, 2, T], F32, name="late_old", tag="x_codes0", align_bytes=64)
         old.extend([late_old[:, 0, :], late_old[:, 1, :]])
         look_up(2)
         look_up(3)

@@ -64,10 +64,10 @@ def tile_picked_widxput_gate_lo_kernel(tc, x_words, x_scales, mem, w1, slot, out
         make_identity(nc, ident[:])
 
         nc.sync.dma_start(w_raw[0][:], w_rows[:, :, :HALF])
-        for q in range(4):
-            nc.sync.dma_start(x_plane[32 * q : 32 * q + 4, :].bitcast(I32), x_scales[0][4 * q : 4 * q + 4, :].bitcast(I32))
         nc.sync.dma_start(offsets[:], slot)
         nc.sync.dma_start(store[0][:], mem_of[0])
+        for q in range(4):
+            nc.sync.dma_start(x_plane[32 * q : 32 * q + 4, :].bitcast(I32), x_scales[0][4 * q : 4 * q + 4, :].bitcast(I32))
         nc.sync.dma_start(x_codes[0][:].bitcast(I32), x_in[:, :HALF])
         nc.sync.dma_start(w_raw[1][:], w_rows[:, :, HALF:])
         nc.sync.dma_start(store[1][:], mem_of[1])
@@ -80,8 +80,8 @@ def tile_picked_widxput_gate_lo_kernel(tc, x_words, x_scales, mem, w1, slot, out
                  w_raw[h][:].rearrange("p j (m two) -> p m j two", two=2)[:, :, :, 0])
 
         def cast_odd(copy, h):
-            copy(w_odd[h][:].rearrange("p (u g j) -> p u g j", u=2, j=PACK),
-                 w_raw[h][:].rearrange("p j (g u two) -> p u g j two", u=2, two=2)[:, :, :, :, 1])
+            copy(w_odd[h][:].rearrange("p (u g j) -> p g u j", u=2, j=PACK),
+                 w_raw[h][:].rearrange("p j (g u two) -> p g u j two", u=2, two=2)[:, :, :, :, 1])
 
         def codes(first, width):
             tile, at = (first_codes, first) if first < P else (later_codes, first - P)
@@ -137,7 +137,7 @@ def tile_picked_widxput_gate_lo_kernel(tc, x_words, x_scales, mem, w1, slot, out
         last_gate = keep.tile([P, T], F32, name="last_gate", align_bytes=64)
 
         cast_even(nc.vector.tensor_copy, 0)
-        cast_odd(nc.vector.tensor_copy, 0)
+        cast_odd(nc.scalar.copy, 0)
         quantise(w_even[0][:], 0)
         quantise_odd(0)
         gate_part(first_gate[0][:], 0, 0, HALF, "acc0")

@@ -18,8 +18,8 @@ PACK = 4
 K, T, N, U = 512, 512, 512, 1024
 HALF = 256
 GROUPS = 4
-PIECES = ((0, 512), (512, 256), (768, 256))
-LAST_VECTOR = (288, 256, 0)
+PIECES = ((0, 256), (256, 512), (768, 256))
+LAST_VECTOR = (256, 352, 0)
 LATE = 128
 FLOPS = 2 * K * N * T
 
@@ -127,8 +127,8 @@ def tile_picked_widxput_gate_lo_kernel(tc, x_words, x_scales, mem, w1, slot, out
             words_t = turned[i][:].rearrange("p u h r -> p (u h r)").bitcast(F32)
             for u in range(2):
                 nc.tensor.transpose(bank[:, u, :], words_t[:, u * P : (u + 1) * P], ident[:])
-            tile = woven[max(0, i - 1)]
-            first = HALF if i == 1 else 0
+            tile = woven[(i + 1) // 2]
+            first = HALF if i == 2 else 0
             pairs = bank[:].rearrange("p u c -> p (u c)").bitcast(BF16).rearrange("p (c e) -> p c e", e=2)
             nc.scalar.copy(tile[:, first : first + HALF, 0:PACK:2], pairs)
 

@@ -19,7 +19,7 @@ K, T, N, U = 512, 512, 512, 1024
 HALF = 256
 GROUPS = 4
 PIECES = ((0, 256), (256, 512), (768, 256))
-LAST_VECTOR = (256, 352, 0)
+LAST_VECTOR = (256, 256, 0)
 LATE = 128
 FLOPS = 2 * K * N * T
 

@@ -15,12 +15,13 @@ MULT = mybir.AluOpType.mult
 
 P = 128
 PACK = 4
+STRIPE = 16
+QUADRANTS = 4
 K, T, N, U = 512, 512, 512, 1024
 HALF = 256
-GROUPS = 4
-PIECES = ((0, 256), (256, 512), (768, 256))
-LAST_VECTOR = (256, 256, 0)
-LATE = 128
+QUARTER = U // 4
+PIECES = ((0, QUARTER), (QUARTER, 2 * QUARTER), (3 * QUARTER, QUARTER))
+VECTOR_SHARE = (256, 288, 0)
 FLOPS = 2 * K * N * T
 
 
@@ -30,31 +31,32 @@ def tile_picked_widxput_gate_lo_kernel(tc, x_words, x_scales, mem, w1, slot, out
         keep = ctx.enter_context(tc.tile_pool(name="keep", bufs=1))
         psum = ctx.enter_context(tc.psum_pool(name="psum", bufs=1))
 
-        offsets = keep.tile([P, T // 16], U16, name="offsets")
+        offsets = keep.tile([P, T // STRIPE], U16, name="offsets")
         x_codes = [keep.tile([P, HALF], U32, name="x_codes", tag="x_codes%d" % h, align_bytes=64) for h in range(2)]
         x_plane = keep.tile([P, T], U8, name="x_plane", align_bytes=64)
         w_raw = [keep.tile([P, PACK, HALF], F32, name="w_raw", tag="w_raw%d" % h, align_bytes=64) for h in range(2)]
-        w_even = [keep.tile([P, PACK * P], BF16, name="w_even", tag="w_even%d" % h, align_bytes=64) for h in range(2)]
-        w_odd = [keep.tile([P, PACK * P], BF16, name="w_odd0", align_bytes=64)]
+        w_odd = [keep.tile([P, PACK * P], BF16, name="w_odd", tag="w_odd%d" % h, align_bytes=64) for h in range(2)]
+        w_even = [keep.tile([P, PACK * P], BF16, name="w_even0", align_bytes=64)]
         first_codes = keep.tile([P, P], U32, name="first_codes", tag="first_codes", align_bytes=64)
         later_codes = keep.tile([P, N - P], U32, name="later_codes", align_bytes=64)
         w_plane = keep.tile([P, N], U8, name="w_plane", align_bytes=64)
         store = [keep.tile([P, U], F32, name="store", tag="store%d" % s, align_bytes=64) for s in range(4)]
         early_old = keep.tile([P, 2, T], F32, name="early_old", align_bytes=64)
         old = [early_old[:, 0, :], early_old[:, 1, :]]
-        turned = [keep.tile([P, 2, 2, P], BF16, name="turned%d" % i, align_bytes=64) for i in range(GROUPS)]
+        turned = [keep.tile([P, 2, 2, P], BF16, name="turned%d" % i, align_bytes=64) for i in range(U // QUARTER)]
         woven = [keep.tile([P, width, PACK], BF16, name="woven%d" % first, align_bytes=64) for first, width in PIECES]
         y_codes = keep.tile([P, U], U32, name="y_codes", align_bytes=64)
         y_plane = keep.tile([P, U], U8, name="y_plane", align_bytes=64)
         ident = keep.tile([P, P], F32, name="ident", align_bytes=64)
         warm = keep.tile([P, 2], F32, name="warm")
 
-        mem_even = mem.rearrange("(h p two) c -> p h two c", h=2, two=2)
-        out_even = out_0.rearrange("(h p two) c -> p h two c", h=2, two=2)
-        mem_rows = mem.rearrange("(p t) c -> p t c", t=PACK)
-        out_rows = out_0.rearrange("(p t) c -> p t c", t=PACK)
-        mem_of = [mem_even[:, 0, 0, :], mem_even[:, 1, 0, :], mem_rows[:, 1, :], mem_rows[:, 3, :]]
-        out_of = [out_even[:, 0, 0, :], out_even[:, 1, 0, :], out_rows[:, 1, :], out_rows[:, 3, :]]
+        def tile_rows(dram):
+            halves = dram.rearrange("(h p two) c -> p h two c", h=2, two=2)
+            lanes = dram.rearrange("(p t) c -> p t c", t=PACK)
+            return [halves[:, 0, 1, :], halves[:, 1, 1, :], lanes[:, 0, :], lanes[:, 2, :]]
+
+        mem_rows = tile_rows(mem)
+        out_rows = tile_rows(out_0)
         w_rows = w1.rearrange("(p j) c -> p j c", j=PACK)
         x_in = x_words[0].rearrange("p c r -> p (c r)").bitcast(I32)
 
@@ -65,57 +67,54 @@ def tile_picked_widxput_gate_lo_kernel(tc, x_words, x_scales, mem, w1, slot, out
 
         nc.sync.dma_start(w_raw[0][:], w_rows[:, :, :HALF])
         nc.sync.dma_start(offsets[:], slot)
-        nc.sync.dma_start(store[0][:], mem_of[0])
-        for q in range(4):
+        nc.sync.dma_start(store[0][:], mem_rows[0])
+        for q in range(QUADRANTS):
             nc.sync.dma_start(x_plane[32 * q : 32 * q + 4, :].bitcast(I32), x_scales[0][4 * q : 4 * q + 4, :].bitcast(I32))
         nc.sync.dma_start(x_codes[0][:].bitcast(I32), x_in[:, :HALF])
         nc.sync.dma_start(w_raw[1][:], w_rows[:, :, HALF:])
-        nc.sync.dma_start(store[1][:], mem_of[1])
+        nc.sync.dma_start(store[1][:], mem_rows[1])
         nc.sync.dma_start(x_codes[1][:].bitcast(I32), x_in[:, HALF:])
-        for step in (2, 3):
-            nc.sync.dma_start(store[step][:], mem_of[step])
-
-        def cast_even(copy, h):
-            copy(w_even[h][:].rearrange("p (m j) -> p m j", j=PACK),
-                 w_raw[h][:].rearrange("p j (m two) -> p m j two", two=2)[:, :, :, 0])
+        for s in (2, 3):
+            nc.sync.dma_start(store[s][:], mem_rows[s])
 
         def cast_odd(copy, h):
-            copy(w_odd[h][:].rearrange("p (u g j) -> p g u j", u=2, j=PACK),
-                 w_raw[h][:].rearrange("p j (g u two) -> p g u j two", u=2, two=2)[:, :, :, :, 1])
+            copy(w_odd[h][:].rearrange("p (m j) -> p m j", j=PACK),
+                 w_raw[h][:].rearrange("p j (m two) -> p m j two", two=2)[:, :, :, 1])
 
-        def codes(first, width):
+        def cast_even(h):
+            nc.scalar.copy(w_even[h][:].rearrange("p (u g j) -> p g u j", u=2, j=PACK),
+                           w_raw[h][:].rearrange("p j (g u two) -> p g u j two", u=2, two=2)[:, :, :, :, 0])
+
+        def w_codes(first, width):
             tile, at = (first_codes, first) if first < P else (later_codes, first - P)
             return tile[:, at : at + width].bitcast(FP8X4)
 
-        def quantise(src, first):
+        def quantise_w(src, first):
             width = src.shape[1] // PACK
-            nc.vector.quantize_mx(out=codes(first, width), scales=w_plane[:, first : first + width], in_=src)
+            nc.vector.quantize_mx(out=w_codes(first, width), scales=w_plane[:, first : first + width], in_=src)
 
-        def quantise_odd(h):
+        def quantise_even(h):
+            run = PACK * P // 2
             for u in range(2):
-                quantise(w_odd[h][:, u * HALF : (u + 1) * HALF], (2 + u) * P + h * P // 2)
+                quantise_w(w_even[h][:, u * run : (u + 1) * run], (2 + u) * P + h * P // 2)
 
-        def gate_part(gate, step, first, width, bank):
-            cols = slice(step * P, (step + 1) * P)
-            acc = psum.tile([P, width], F32, name="acc", tag=bank)
-            for at in range(first, first + width, HALF):
-                wide = min(HALF, first + width - at)
-                nc.tensor.matmul_mx(out=acc[:, at - first : at - first + wide], lhsT=codes(step * P, P),
-                                    lhsT_scale=w_plane[:, cols],
-                                    rhs=x_codes[at // HALF][:, at % HALF : at % HALF + wide].bitcast(FP8X4),
-                                    rhs_scale=x_plane[:, at : at + wide], start=True, stop=True)
+        def make_gate(gate, s, x_halves, bank):
+            acc = psum.tile([P, len(x_halves) * HALF], F32, name="acc", tag=bank)
+            for n, h in enumerate(x_halves):
+                nc.tensor.matmul_mx(out=acc[:, n * HALF : (n + 1) * HALF], lhsT=w_codes(s * P, P),
+                                    lhsT_scale=w_plane[:, s * P : (s + 1) * P], rhs=x_codes[h][:].bitcast(FP8X4),
+                                    rhs_scale=x_plane[:, h * HALF : (h + 1) * HALF], start=True, stop=True)
             nc.scalar.activation(gate, acc[:], SIGMOID)
 
-        def look_up(step):
-            nc.vector.tensor_copy(old[step], store[step][:].indirect(offsets[:]))
+        def look_up(s):
+            nc.vector.tensor_copy(old[s], store[s][:].indirect(offsets[:]))
 
-        def put(step, gate, first, width):
-            part = slice(first, first + width)
-            nc.vector.tensor_tensor(store[step][:].indirect(offsets[:, first // 16 : (first + width) // 16]),
-                                    old[step][:, part], gate, MULT)
+        def put(s, gate, first, count):
+            nc.vector.tensor_tensor(store[s][:].indirect(offsets[:, first // STRIPE : (first + count) // STRIPE]),
+                                    old[s][:, first : first + count], gate, MULT)
 
         def turn(h):
-            for i in range(GROUPS):
+            for i in range(len(turned)):
                 bank = psum.tile([P, 2, P], F32, name="bank", tag="turn%d" % i)
                 for u in range(2):
                     block = 2 * i + u
@@ -124,69 +123,72 @@ def tile_picked_widxput_gate_lo_kernel(tc, x_words, x_scales, mem, w1, slot, out
 
         def turn_back(i):
             bank = psum.tile([P, 2, P], F32, name="bank", tag="turn%d" % i)
-            words_t = turned[i][:].rearrange("p u h r -> p (u h r)").bitcast(F32)
+            pair_words = turned[i][:].rearrange("p u h r -> p (u h r)").bitcast(F32)
             for u in range(2):
-                nc.tensor.transpose(bank[:, u, :], words_t[:, u * P : (u + 1) * P], ident[:])
-            tile = woven[(i + 1) // 2]
-            first = HALF if i == 2 else 0
-            pairs = bank[:].rearrange("p u c -> p (u c)").bitcast(BF16).rearrange("p (c e) -> p c e", e=2)
-            nc.scalar.copy(tile[:, first : first + HALF, 0:PACK:2], pairs)
+                nc.tensor.transpose(bank[:, u, :], pair_words[:, u * P : (u + 1) * P], ident[:])
+            pairs = bank[:].rearrange("p u c -> p (u c)").bitcast(BF16)
+            for tile, (first, width) in zip(woven, PIECES):
+                at = i * QUARTER - first
+                if 0 <= at < width:
+                    nc.scalar.copy(tile[:, at : at + QUARTER, :].rearrange("p c t -> p (c t)").bitcast(F32), pairs)
 
         first_gate = [keep.tile([P, HALF], F32, name="first_gate", tag="first_gate%d" % h, align_bytes=64) for h in range(2)]
         second_gate = keep.tile([P, T], F32, name="second_gate", align_bytes=64)
         last_gate = keep.tile([P, T], F32, name="last_gate", align_bytes=64)
 
-        cast_even(nc.vector.tensor_copy, 0)
-        cast_odd(nc.scalar.copy, 0)
-        quantise(w_even[0][:], 0)
-        quantise_odd(0)
-        gate_part(first_gate[0][:], 0, 0, HALF, "acc0")
+        cast_odd(nc.vector.tensor_copy, 0)
+        cast_even(0)
+        quantise_w(w_odd[0][:], 0)
+        quantise_even(0)
+        make_gate(first_gate[0][:], 0, (0,), "acc0")
         look_up(0)
         look_up(1)
         put(0, first_gate[0][:], 0, HALF)
-        cast_even(nc.scalar.copy, 1)
-        gate_part(first_gate[1][:], 0, HALF, HALF, "acc1")
-        w_odd.append(keep.tile([P, PACK * P], BF16, name="w_odd1", tag="first_codes", align_bytes=64))
         cast_odd(nc.scalar.copy, 1)
-        quantise(w_even[1][:], P)
+        make_gate(first_gate[1][:], 0, (1,), "acc1")
+        w_even.append(keep.tile([P, PACK * P], BF16, name="w_even1", tag="first_codes", align_bytes=64))
+        cast_even(1)
+        quantise_w(w_odd[1][:], P)
         put(0, first_gate[1][:], HALF, HALF)
-        nc.sync.dma_start(out_of[0], store[0][:])
-        gate_part(second_gate[:], 1, 0, T, "acc1")
-        quantise_odd(1)
+        nc.sync.dma_start(out_rows[0], store[0][:])
+
+        make_gate(second_gate[:], 1, (0, 1), "acc1")
+        quantise_even(1)
         turn(0)
-        gate_part(last_gate[:, :HALF], 3, 0, HALF, "acc0")
-        gate_part(last_gate[:, HALF : T - LATE], 3, HALF, LATE, "acc2")
-        put(1, second_gate[:], 0, T)
-        nc.sync.dma_start(out_of[1], store[1][:])
         third_gate = keep.tile([P, T], F32, name="third_gate", align_bytes=64)
-        gate_part(third_gate[:], 2, 0, T, "acc1")
+        make_gate(third_gate[:], 2, (0, 1), "acc0")
+        put(1, second_gate[:], 0, T)
+        nc.sync.dma_start(out_rows[1], store[1][:])
+
+        make_gate(last_gate[:, :HALF], 3, (0,), "acc1")
         late_old = keep.tile([P, 2, T], F32, name="late_old", tag="x_codes0", align_bytes=64)
         old.extend([late_old[:, 0, :], late_old[:, 1, :]])
         look_up(2)
         look_up(3)
         turn(1)
-        for i in range(GROUPS):
+        for i in range(len(turned)):
             turn_back(i)
-            if i == 2:
-                gate_part(last_gate[:, T - LATE :], 3, T - LATE, LATE, "turn0")
+        make_gate(last_gate[:, HALF:], 3, (1,), "turn0")
+
         put(2, third_gate[:], 0, T)
-        nc.sync.dma_start(out_of[2], store[2][:])
+        nc.sync.dma_start(out_rows[2], store[2][:])
         for tile, (first, width) in zip(woven, PIECES):
-            nc.scalar.copy(tile[:, :, 1], store[2][:, first : first + width])
+            nc.scalar.copy(tile[:, :, 0], store[2][:, first : first + width])
         put(3, last_gate[:], 0, T)
-        nc.sync.dma_start(out_of[3], store[3][:])
-        for tile, (first, width), share in zip(woven, PIECES, LAST_VECTOR):
+        nc.sync.dma_start(out_rows[3], store[3][:])
+        for tile, (first, width), share in zip(woven, PIECES, VECTOR_SHARE):
             src = store[3][:, first : first + width]
             if share:
-                nc.vector.tensor_copy(tile[:, :share, 3], src[:, :share])
+                nc.vector.tensor_copy(tile[:, :share, 2], src[:, :share])
             if share < width:
-                nc.scalar.copy(tile[:, share:, 3], src[:, share:])
+                nc.scalar.copy(tile[:, share:, 2], src[:, share:])
 
-        words = out_1[0].rearrange("p c r -> p (c r)").bitcast(I32)
+        out_words = out_1[0].rearrange("p c r -> p (c r)").bitcast(I32)
         for tile, (first, width) in zip(woven, PIECES):
             cols = slice(first, first + width)
             nc.vector.quantize_mx(out=y_codes[:, cols].bitcast(FP8X4), scales=y_plane[:, cols],
                                   in_=tile[:].rearrange("p c t -> p (c t)"))
-            nc.sync.dma_start(words[:, cols], y_codes[:, cols].bitcast(I32))
-        for q in range(4):
-            (nc.sync if q == 0 else nc.scalar).dma_start(out_2[0][4 * q : 4 * q + 4, :].bitcast(I32), y_plane[32 * q : 32 * q + 4, :].bitcast(I32))
+            nc.sync.dma_start(out_words[:, cols], y_codes[:, cols].bitcast(I32))
+        for q in range(QUADRANTS):
+            queue = nc.sync if q == 0 else nc.scalar
+            queue.dma_start(out_2[0][4 * q : 4 * q + 4, :].bitcast(I32), y_plane[32 * q : 32 * q + 4, :].bitcast(I32))

@@ -190,5 +190,4 @@ def tile_picked_widxput_gate_lo_kernel(tc, x_words, x_scales, mem, w1, slot, out
                                   in_=tile[:].rearrange("p c t -> p (c t)"))
             nc.sync.dma_start(out_words[:, cols], y_codes[:, cols].bitcast(I32))
         for q in range(QUADRANTS):
-            queue = nc.sync if q == 0 else nc.scalar
-            queue.dma_start(out_2[0][4 * q : 4 * q + 4, :].bitcast(I32), y_plane[32 * q : 32 * q + 4, :].bitcast(I32))
+            nc.sync.dma_start(out_2[0][4 * q : 4 * q + 4, :].bitcast(I32), y_plane[32 * q : 32 * q + 4, :].bitcast(I32))

@@ -1,7 +1,6 @@
 from contextlib import ExitStack
 
 import concourse.mybir as mybir
-from concourse.masks import make_identity
 
 F32 = mybir.dt.float32
 BF16 = mybir.dt.bfloat16
@@ -11,6 +10,7 @@ U16 = mybir.dt.uint16
 U8 = mybir.dt.uint8
 FP8X4 = mybir.dt.float8_e4m3fn_x4
 SIGMOID = mybir.ActivationFunctionType.Sigmoid
+COPY = mybir.ActivationFunctionType.Copy
 MULT = mybir.AluOpType.mult
 
 P = 128
@@ -19,9 +19,11 @@ STRIPE = 16
 QUADRANTS = 4
 K, T, N, U = 512, 512, 512, 1024
 HALF = 256
-QUARTER = U // 4
-PIECES = ((0, QUARTER), (QUARTER, 2 * QUARTER), (3 * QUARTER, QUARTER))
-VECTOR_SHARE = (256, 288, 0)
+GROUPS = HALF // PACK
+PIECES = ((0, 256), (256, 384), (640, 384))
+W_FIRST = 384
+W_SCALAR = 10
+VECTOR_PUTS = 128
 FLOPS = 2 * K * N * T
 
 
@@ -32,162 +34,116 @@ def tile_picked_widxput_gate_lo_kernel(tc, x_words, x_scales, mem, w1, slot, out
         psum = ctx.enter_context(tc.psum_pool(name="psum", bufs=1))
 
         offsets = keep.tile([P, T // STRIPE], U16, name="offsets")
-        x_codes = [keep.tile([P, HALF], U32, name="x_codes", tag="x_codes%d" % h, align_bytes=64) for h in range(2)]
+        x_codes = keep.tile([P, T], U32, name="x_codes", align_bytes=64)
         x_plane = keep.tile([P, T], U8, name="x_plane", align_bytes=64)
-        w_raw = [keep.tile([P, PACK, HALF], F32, name="w_raw", tag="w_raw%d" % h, align_bytes=64) for h in range(2)]
-        w_odd = [keep.tile([P, PACK * P], BF16, name="w_odd", tag="w_odd%d" % h, align_bytes=64) for h in range(2)]
-        w_even = [keep.tile([P, PACK * P], BF16, name="w_even0", align_bytes=64)]
-        first_codes = keep.tile([P, P], U32, name="first_codes", tag="first_codes", align_bytes=64)
-        later_codes = keep.tile([P, N - P], U32, name="later_codes", align_bytes=64)
+        w_raw = [keep.tile([P, PACK, width], F32, name="w_raw%d" % width, align_bytes=64) for width in (W_FIRST, N - W_FIRST)]
+        w_dealt = [keep.tile([P, PACK, GROUPS, PACK], BF16, name="w_dealt%d" % h, align_bytes=64) for h in range(2)]
+        w_codes = keep.tile([P, N], U32, name="w_codes", align_bytes=64)
         w_plane = keep.tile([P, N], U8, name="w_plane", align_bytes=64)
-        store = [keep.tile([P, U], F32, name="store", tag="store%d" % s, align_bytes=64) for s in range(4)]
-        early_old = keep.tile([P, 2, T], F32, name="early_old", align_bytes=64)
-        old = [early_old[:, 0, :], early_old[:, 1, :]]
-        turned = [keep.tile([P, 2, 2, P], BF16, name="turned%d" % i, align_bytes=64) for i in range(U // QUARTER)]
-        woven = [keep.tile([P, width, PACK], BF16, name="woven%d" % first, align_bytes=64) for first, width in PIECES]
+        store = [keep.tile([P, U], F32, name="store%d" % s, align_bytes=64) for s in range(4)]
+        gate = [keep.tile([P, T], F32, name="gate%d" % s, align_bytes=64) for s in range(4)]
+        new = [keep.tile([P, T], F32, name="new%d" % s, align_bytes=64) for s in range(3)]
+        old = keep.tile([P, T], F32, name="old", tag="pairs", align_bytes=64)
+        woven = [keep.tile([P, width, 2], I32, name="woven%d" % first, align_bytes=64) for first, width in PIECES]
         y_codes = keep.tile([P, U], U32, name="y_codes", align_bytes=64)
         y_plane = keep.tile([P, U], U8, name="y_plane", align_bytes=64)
-        ident = keep.tile([P, P], F32, name="ident", align_bytes=64)
         warm = keep.tile([P, 2], F32, name="warm")
 
-        def tile_rows(dram):
-            halves = dram.rearrange("(h p two) c -> p h two c", h=2, two=2)
-            lanes = dram.rearrange("(p t) c -> p t c", t=PACK)
-            return [halves[:, 0, 1, :], halves[:, 1, 1, :], lanes[:, 0, :], lanes[:, 2, :]]
-
-        mem_rows = tile_rows(mem)
-        out_rows = tile_rows(out_0)
+        lanes = (0, 2, 3, 1)
+        mem_rows = mem.rearrange("(p t) c -> p t c", t=PACK)
+        out_rows = out_0.rearrange("(p t) c -> p t c", t=PACK)
         w_rows = w1.rearrange("(p j) c -> p j c", j=PACK)
-        x_in = x_words[0].rearrange("p c r -> p (c r)").bitcast(I32)
 
         nc.vector.memset(x_plane[:].bitcast(I32), 0)
         nc.vector.memset(warm[:, 0:1], 0.0)
         nc.scalar.activation(warm[:, 1:2], warm[:, 0:1], SIGMOID)
-        make_identity(nc, ident[:])
 
-        nc.sync.dma_start(w_raw[0][:], w_rows[:, :, :HALF])
         nc.sync.dma_start(offsets[:], slot)
-        nc.sync.dma_start(store[0][:], mem_rows[0])
+        nc.sync.dma_start(w_raw[0][:], w_rows[:, :, :W_FIRST])
+        nc.sync.dma_start(w_raw[1][:], w_rows[:, :, W_FIRST:])
         for q in range(QUADRANTS):
             nc.sync.dma_start(x_plane[32 * q : 32 * q + 4, :].bitcast(I32), x_scales[0][4 * q : 4 * q + 4, :].bitcast(I32))
-        nc.sync.dma_start(x_codes[0][:].bitcast(I32), x_in[:, :HALF])
-        nc.sync.dma_start(w_raw[1][:], w_rows[:, :, HALF:])
-        nc.sync.dma_start(store[1][:], mem_rows[1])
-        nc.sync.dma_start(x_codes[1][:].bitcast(I32), x_in[:, HALF:])
-        for s in (2, 3):
-            nc.sync.dma_start(store[s][:], mem_rows[s])
+        nc.sync.dma_start(x_codes[:].bitcast(I32), x_words[0].rearrange("p c r -> p (c r)").bitcast(I32))
+        for s in range(4):
+            nc.sync.dma_start(store[s][:], mem_rows[:, lanes[s], :])
 
-        def cast_odd(copy, h):
-            copy(w_odd[h][:].rearrange("p (m j) -> p m j", j=PACK),
-                 w_raw[h][:].rearrange("p j (m two) -> p m j two", two=2)[:, :, :, 1])
+        def round_w(copy, first, last):
+            h, at = divmod(first, GROUPS)
+            raw, start = (w_raw[0], first) if first < W_FIRST // PACK else (w_raw[1], first - W_FIRST // PACK)
+            copy(w_dealt[h][:, :, at : at + last - first, :].rearrange("p t g j -> p g t j"),
+                 raw[:].rearrange("p j (g t) -> p g t j", t=PACK)[:, start : start + last - first])
 
-        def cast_even(h):
-            nc.scalar.copy(w_even[h][:].rearrange("p (u g j) -> p g u j", u=2, j=PACK),
-                           w_raw[h][:].rearrange("p j (g u two) -> p g u j two", u=2, two=2)[:, :, :, :, 0])
+        def quantise_w(h):
+            for s in range(4):
+                at = lanes[s] * P + h * GROUPS
+                nc.vector.quantize_mx(out=w_codes[:, at : at + GROUPS].bitcast(FP8X4), scales=w_plane[:, at : at + GROUPS],
+                                      in_=w_dealt[h][:, lanes[s]].rearrange("p g j -> p (g j)"))
 
-        def w_codes(first, width):
-            tile, at = (first_codes, first) if first < P else (later_codes, first - P)
-            return tile[:, at : at + width].bitcast(FP8X4)
+        round_w(nc.vector.tensor_copy, 0, GROUPS)
+        round_w(nc.scalar.copy, GROUPS, W_FIRST // PACK)
+        round_w(nc.vector.tensor_copy, W_FIRST // PACK, P - W_SCALAR)
+        round_w(nc.scalar.copy, P - W_SCALAR, P)
+        quantise_w(1)
+        quantise_w(0)
 
-        def quantise_w(src, first):
-            width = src.shape[1] // PACK
-            nc.vector.quantize_mx(out=w_codes(first, width), scales=w_plane[:, first : first + width], in_=src)
+        def make_gate(s, first, width):
+            acc = psum.tile([P, width], F32, name="acc%d_%d" % (s, first))
+            cols = slice(lanes[s] * P, (lanes[s] + 1) * P)
+            nc.tensor.matmul_mx(out=acc[:], lhsT=w_codes[:, cols].bitcast(FP8X4), lhsT_scale=w_plane[:, cols],
+                                rhs=x_codes[:, first : first + width].bitcast(FP8X4),
+                                rhs_scale=x_plane[:, first : first + width], start=True, stop=True)
+            nc.scalar.activation(gate[s][:, first : first + width], acc[:], SIGMOID)
 
-        def quantise_even(h):
-            run = PACK * P // 2
-            for u in range(2):
-                quantise_w(w_even[h][:, u * run : (u + 1) * run], (2 + u) * P + h * P // 2)
+        make_gate(0, 0, HALF)
+        make_gate(0, HALF, HALF)
+        for s in range(1, 4):
+            make_gate(s, 0, T)
 
-        def make_gate(gate, s, x_halves, bank):
-            acc = psum.tile([P, len(x_halves) * HALF], F32, name="acc", tag=bank)
-            for n, h in enumerate(x_halves):
-                nc.tensor.matmul_mx(out=acc[:, n * HALF : (n + 1) * HALF], lhsT=w_codes(s * P, P),
-                                    lhsT_scale=w_plane[:, s * P : (s + 1) * P], rhs=x_codes[h][:].bitcast(FP8X4),
-                                    rhs_scale=x_plane[:, h * HALF : (h + 1) * HALF], start=True, stop=True)
-            nc.scalar.activation(gate, acc[:], SIGMOID)
+        for h in range(2):
+            cols = slice(h * HALF, (h + 1) * HALF)
+            nc.vector.tensor_tensor(new[0][:, cols], store[0][:].indirect(offsets[:, h * HALF // STRIPE : (h + 1) * HALF // STRIPE]),
+                                    gate[0][:, cols], MULT)
+        for s in (1, 2):
+            nc.vector.tensor_tensor(new[s][:], store[s][:].indirect(offsets[:]), gate[s][:], MULT)
+        nc.vector.tensor_copy(store[2][:].indirect(offsets[:, : VECTOR_PUTS // STRIPE]), new[2][:, :VECTOR_PUTS])
+        nc.vector.tensor_copy(old[:], store[3][:].indirect(offsets[:]))
+        nc.vector.tensor_tensor(store[3][:].indirect(offsets[:]), old[:], gate[3][:], MULT)
 
-        def look_up(s):
-            nc.vector.tensor_copy(old[s], store[s][:].indirect(offsets[:]))
+        def put(s, first, last):
+            nc.scalar.activation(store[s][:].indirect(offsets[:, first // STRIPE : last // STRIPE]), new[s][:, first:last], COPY)
 
-        def put(s, gate, first, count):
-            nc.vector.tensor_tensor(store[s][:].indirect(offsets[:, first // STRIPE : (first + count) // STRIPE]),
-                                    old[s][:, first : first + count], gate, MULT)
+        for s in range(2):
+            put(s, 0, HALF)
+            put(s, HALF, T)
+        put(2, VECTOR_PUTS, T)
+        for s in (0, 3, 1, 2):
+            nc.sync.dma_start(out_rows[:, lanes[s], :], store[s][:])
 
-        def turn(h):
-            for i in range(len(turned)):
-                bank = psum.tile([P, 2, P], F32, name="bank", tag="turn%d" % i)
-                for u in range(2):
-                    block = 2 * i + u
-                    nc.tensor.transpose(bank[:, u, :], store[h][:, block * P : (block + 1) * P], ident[:])
-                nc.scalar.copy(turned[i][:, :, h, :], bank[:])
+        pairs = keep.tile([P, 2, U, 2], BF16, name="pairs", tag="pairs", align_bytes=64)
+        pair_words = pairs[:].rearrange("p u c e -> p u (c e)").bitcast(I32)
 
-        def turn_back(i):
-            bank = psum.tile([P, 2, P], F32, name="bank", tag="turn%d" % i)
-            pair_words = turned[i][:].rearrange("p u h r -> p (u h r)").bitcast(F32)
-            for u in range(2):
-                nc.tensor.transpose(bank[:, u, :], pair_words[:, u * P : (u + 1) * P], ident[:])
-            pairs = bank[:].rearrange("p u c -> p (u c)").bitcast(BF16)
-            for tile, (first, width) in zip(woven, PIECES):
-                at = i * QUARTER - first
-                if 0 <= at < width:
-                    nc.scalar.copy(tile[:, at : at + QUARTER, :].rearrange("p c t -> p (c t)").bitcast(F32), pairs)
+        def round_lane(copy, s, first, width):
+            copy(pairs[:, lanes[s] // 2, first : first + width, lanes[s] % 2], store[s][:, first : first + width])
 
-        first_gate = [keep.tile([P, HALF], F32, name="first_gate", tag="first_gate%d" % h, align_bytes=64) for h in range(2)]
-        second_gate = keep.tile([P, T], F32, name="second_gate", align_bytes=64)
-        last_gate = keep.tile([P, T], F32, name="last_gate", align_bytes=64)
-
-        cast_odd(nc.vector.tensor_copy, 0)
-        cast_even(0)
-        quantise_w(w_odd[0][:], 0)
-        quantise_even(0)
-        make_gate(first_gate[0][:], 0, (0,), "acc0")
-        look_up(0)
-        look_up(1)
-        put(0, first_gate[0][:], 0, HALF)
-        cast_odd(nc.scalar.copy, 1)
-        make_gate(first_gate[1][:], 0, (1,), "acc1")
-        w_even.append(keep.tile([P, PACK * P], BF16, name="w_even1", tag="first_codes", align_bytes=64))
-        cast_even(1)
-        quantise_w(w_odd[1][:], P)
-        put(0, first_gate[1][:], HALF, HALF)
-        nc.sync.dma_start(out_rows[0], store[0][:])
-
-        make_gate(second_gate[:], 1, (0, 1), "acc1")
-        quantise_even(1)
-        turn(0)
-        third_gate = keep.tile([P, T], F32, name="third_gate", align_bytes=64)
-        make_gate(third_gate[:], 2, (0, 1), "acc0")
-        put(1, second_gate[:], 0, T)
-        nc.sync.dma_start(out_rows[1], store[1][:])
-
-        make_gate(last_gate[:, :HALF], 3, (0,), "acc1")
-        late_old = keep.tile([P, 2, T], F32, name="late_old", tag="x_codes0", align_bytes=64)
-        old.extend([late_old[:, 0, :], late_old[:, 1, :]])
-        look_up(2)
-        look_up(3)
-        turn(1)
-        for i in range(len(turned)):
-            turn_back(i)
-        make_gate(last_gate[:, HALF:], 3, (1,), "turn0")
-
-        put(2, third_gate[:], 0, T)
-        nc.sync.dma_start(out_rows[2], store[2][:])
-        for tile, (first, width) in zip(woven, PIECES):
-            nc.scalar.copy(tile[:, :, 0], store[2][:, first : first + width])
-        put(3, last_gate[:], 0, T)
-        nc.sync.dma_start(out_rows[3], store[3][:])
-        for tile, (first, width), share in zip(woven, PIECES, VECTOR_SHARE):
-            src = store[3][:, first : first + width]
-            if share:
-                nc.vector.tensor_copy(tile[:, :share, 2], src[:, :share])
-            if share < width:
-                nc.scalar.copy(tile[:, share:, 2], src[:, share:])
-
+        split, rest = PIECES[-1]
+        for s in (0, 3):
+            round_lane(nc.vector.tensor_copy, s, 0, U)
+        round_lane(nc.vector.tensor_copy, 1, 0, split)
+        for s in (1, 2):
+            round_lane(nc.scalar.copy, s, split, rest)
+        for first, width in PIECES[:-1]:
+            round_lane(nc.vector.tensor_copy, 2, first, width)
         out_words = out_1[0].rearrange("p c r -> p (c r)").bitcast(I32)
+        for tile, (first, width) in zip(woven, PIECES):
+            src = pair_words[:, :, first : first + width].rearrange("p u c -> p c u")
+            if first == split:
+                nc.scalar.copy(tile[:].bitcast(U32), src.bitcast(U32))
+            else:
+                nc.vector.tensor_copy(tile[:], src)
         for tile, (first, width) in zip(woven, PIECES):
             cols = slice(first, first + width)
             nc.vector.quantize_mx(out=y_codes[:, cols].bitcast(FP8X4), scales=y_plane[:, cols],
-                                  in_=tile[:].rearrange("p c t -> p (c t)"))
+                                  in_=tile[:].rearrange("p c u -> p (c u)").bitcast(BF16))
             nc.sync.dma_start(out_words[:, cols], y_codes[:, cols].bitcast(I32))
         for q in range(QUADRANTS):
             nc.sync.dma_start(out_2[0][4 * q : 4 * q + 4, :].bitcast(I32), y_plane[32 * q : 32 * q + 4, :].bitcast(I32))

@@ -12,6 +12,7 @@ FP8X4 = mybir.dt.float8_e4m3fn_x4
 SIGMOID = mybir.ActivationFunctionType.Sigmoid
 COPY = mybir.ActivationFunctionType.Copy
 MULT = mybir.AluOpType.mult
+ADD = mybir.AluOpType.add
 
 P = 128
 PACK = 4
@@ -23,7 +24,7 @@ GROUPS = HALF // PACK
 PIECES = ((0, 256), (256, 384), (640, 384))
 W_FIRST = 384
 W_SCALAR = 10
-VECTOR_PUTS = 128
+VECTOR_PUTS = 320
 FLOPS = 2 * K * N * T
 
 
@@ -41,15 +42,14 @@ def tile_picked_widxput_gate_lo_kernel(tc, x_words, x_scales, mem, w1, slot, out
         w_codes = keep.tile([P, N], U32, name="w_codes", align_bytes=64)
         w_plane = keep.tile([P, N], U8, name="w_plane", align_bytes=64)
         store = [keep.tile([P, U], F32, name="store%d" % s, align_bytes=64) for s in range(4)]
-        gate = [keep.tile([P, T], F32, name="gate%d" % s, align_bytes=64) for s in range(4)]
-        new = [keep.tile([P, T], F32, name="new%d" % s, align_bytes=64) for s in range(3)]
-        old = keep.tile([P, T], F32, name="old", tag="pairs", align_bytes=64)
+        gate = [keep.tile([P, T], F32, name="gate", tag="gate%d" % s, align_bytes=64) for s in range(4)]
+        new = [keep.tile([P, T], F32, name="new%d" % s, align_bytes=64) for s in range(4)]
         woven = [keep.tile([P, width, 2], I32, name="woven%d" % first, align_bytes=64) for first, width in PIECES]
         y_codes = keep.tile([P, U], U32, name="y_codes", align_bytes=64)
         y_plane = keep.tile([P, U], U8, name="y_plane", align_bytes=64)
         warm = keep.tile([P, 2], F32, name="warm")
 
-        lanes = (0, 2, 3, 1)
+        lanes = (0, 1, 2, 3)
         mem_rows = mem.rearrange("(p t) c -> p t c", t=PACK)
         out_rows = out_0.rearrange("(p t) c -> p t c", t=PACK)
         w_rows = w1.rearrange("(p j) c -> p j c", j=PACK)
@@ -99,40 +99,49 @@ def tile_picked_widxput_gate_lo_kernel(tc, x_words, x_scales, mem, w1, slot, out
         for s in range(1, 4):
             make_gate(s, 0, T)
 
-        for h in range(2):
-            cols = slice(h * HALF, (h + 1) * HALF)
-            nc.vector.tensor_tensor(new[0][:, cols], store[0][:].indirect(offsets[:, h * HALF // STRIPE : (h + 1) * HALF // STRIPE]),
-                                    gate[0][:, cols], MULT)
-        for s in (1, 2):
-            nc.vector.tensor_tensor(new[s][:], store[s][:].indirect(offsets[:]), gate[s][:], MULT)
-        nc.vector.tensor_copy(store[2][:].indirect(offsets[:, : VECTOR_PUTS // STRIPE]), new[2][:, :VECTOR_PUTS])
-        nc.vector.tensor_copy(old[:], store[3][:].indirect(offsets[:]))
-        nc.vector.tensor_tensor(store[3][:].indirect(offsets[:]), old[:], gate[3][:], MULT)
+        def entries(first, last):
+            return offsets[:, first // STRIPE : last // STRIPE]
+
+        def look_up(s, first, last):
+            nc.vector.tensor_tensor(new[s][:, first:last], store[s][:].indirect(entries(first, last)), gate[s][:, first:last], MULT)
+
+        look_up(0, 0, HALF)
+        look_up(0, HALF, T)
+        look_up(1, 0, VECTOR_PUTS)
+        look_up(1, VECTOR_PUTS, T)
+        nc.vector.tensor_copy(store[1][:].indirect(entries(0, VECTOR_PUTS)), new[1][:, :VECTOR_PUTS])
+        look_up(2, 0, T)
+        look_up(3, 0, T)
+        nc.vector.tensor_copy(store[3][:].indirect(offsets[:]), new[3][:])
 
         def put(s, first, last):
-            nc.scalar.activation(store[s][:].indirect(offsets[:, first // STRIPE : last // STRIPE]), new[s][:, first:last], COPY)
+            nc.scalar.activation(store[s][:].indirect(entries(first, last)), new[s][:, first:last], COPY)
 
-        for s in range(2):
-            put(s, 0, HALF)
-            put(s, HALF, T)
-        put(2, VECTOR_PUTS, T)
-        for s in (0, 3, 1, 2):
+        put(0, 0, HALF)
+        put(0, HALF, T)
+        put(1, VECTOR_PUTS, T)
+        put(2, 0, HALF)
+        put(2, HALF, T)
+        for s in range(4):
             nc.sync.dma_start(out_rows[:, lanes[s], :], store[s][:])
 
-        pairs = keep.tile([P, 2, U, 2], BF16, name="pairs", tag="pairs", align_bytes=64)
+        pairs = keep.tile([P, 2, U, 2], BF16, name="pairs", tag="gate3", align_bytes=64)
         pair_words = pairs[:].rearrange("p u c e -> p u (c e)").bitcast(I32)
 
         def round_lane(copy, s, first, width):
             copy(pairs[:, lanes[s] // 2, first : first + width, lanes[s] % 2], store[s][:, first : first + width])
 
+        def pool_copy(dst, src):
+            nc.gpsimd.tensor_scalar(dst, src, 1.0, -0.0, MULT, ADD)
+
         split, rest = PIECES[-1]
-        for s in (0, 3):
-            round_lane(nc.vector.tensor_copy, s, 0, U)
-        round_lane(nc.vector.tensor_copy, 1, 0, split)
-        for s in (1, 2):
+        for s in (0, 1):
+            round_lane(pool_copy, s, 0, U)
+        round_lane(nc.vector.tensor_copy, 2, 0, split)
+        for s in (2, 3):
             round_lane(nc.scalar.copy, s, split, rest)
         for first, width in PIECES[:-1]:
-            round_lane(nc.vector.tensor_copy, 2, first, width)
+            round_lane(nc.vector.tensor_copy, 3, first, width)
         out_words = out_1[0].rearrange("p c r -> p (c r)").bitcast(I32)
         for tile, (first, width) in zip(woven, PIECES):
             src = pair_words[:, :, first : first + width].rearrange("p u c -> p c u")

@@ -43,6 +43,8 @@ def tile_picked_widxput_gate_lo_kernel(tc, x_words, x_scales, mem, w1, slot, out
         w_plane = keep.tile([P, N], U8, name="w_plane", align_bytes=64)
         store = [keep.tile([P, U], F32, name="store%d" % s, align_bytes=64) for s in range(4)]
         gate = [keep.tile([P, T], F32, name="gate", tag="gate%d" % s, align_bytes=64) for s in range(4)]
+        old = keep.tile([P, T], F32, name="old", align_bytes=64)
+        second_old = keep.tile([P, T], F32, name="second_old", align_bytes=64)
         new = [keep.tile([P, T], F32, name="new%d" % s, align_bytes=64) for s in range(4)]
         woven = [keep.tile([P, width, 2], I32, name="woven%d" % first, align_bytes=64) for first, width in PIECES]
         y_codes = keep.tile([P, U], U32, name="y_codes", align_bytes=64)
@@ -105,11 +107,15 @@ def tile_picked_widxput_gate_lo_kernel(tc, x_words, x_scales, mem, w1, slot, out
         def look_up(s, first, last):
             nc.vector.tensor_tensor(new[s][:, first:last], store[s][:].indirect(entries(first, last)), gate[s][:, first:last], MULT)
 
-        look_up(0, 0, HALF)
-        look_up(0, HALF, T)
-        look_up(1, 0, VECTOR_PUTS)
-        look_up(1, VECTOR_PUTS, T)
-        nc.vector.tensor_copy(store[1][:].indirect(entries(0, VECTOR_PUTS)), new[1][:, :VECTOR_PUTS])
+        for first in (0, HALF):
+            cols = slice(first, first + HALF)
+            nc.vector.tensor_copy(old[:, cols], store[0][:].indirect(entries(first, first + HALF)))
+            nc.gpsimd.tensor_tensor(new[0][:, cols], old[:, cols], gate[0][:, cols], MULT)
+        nc.vector.tensor_copy(second_old[:, VECTOR_PUTS:], store[1][:].indirect(entries(VECTOR_PUTS, T)))
+        nc.gpsimd.tensor_tensor(new[1][:, VECTOR_PUTS:], second_old[:, VECTOR_PUTS:], gate[1][:, VECTOR_PUTS:], MULT)
+        nc.vector.tensor_copy(second_old[:, :VECTOR_PUTS], store[1][:].indirect(entries(0, VECTOR_PUTS)))
+        nc.vector.tensor_tensor(store[1][:].indirect(entries(0, VECTOR_PUTS)), second_old[:, :VECTOR_PUTS],
+                                gate[1][:, :VECTOR_PUTS], MULT)
         look_up(2, 0, T)
         look_up(3, 0, T)
         nc.vector.tensor_copy(store[3][:].indirect(offsets[:]), new[3][:])

@@ -24,7 +24,10 @@ GROUPS = HALF // PACK
 PIECES = ((0, 256), (256, 384), (640, 384))
 W_FIRST = 384
 W_SCALAR = 10
-VECTOR_PUTS = 320
+FIRST_CUTS = (0, 128, 256, 512)
+LATE = 64
+SHORT = 128
+SCALAR_PUTS = 288
 FLOPS = 2 * K * N * T
 
 
@@ -42,16 +45,20 @@ def tile_picked_widxput_gate_lo_kernel(tc, x_words, x_scales, mem, w1, slot, out
         w_codes = keep.tile([P, N], U32, name="w_codes", align_bytes=64)
         w_plane = keep.tile([P, N], U8, name="w_plane", align_bytes=64)
         store = [keep.tile([P, U], F32, name="store%d" % s, align_bytes=64) for s in range(4)]
-        gate = [keep.tile([P, T], F32, name="gate", tag="gate%d" % s, align_bytes=64) for s in range(4)]
-        old = keep.tile([P, T], F32, name="old", align_bytes=64)
-        second_old = keep.tile([P, T], F32, name="second_old", align_bytes=64)
-        new = [keep.tile([P, T], F32, name="new%d" % s, align_bytes=64) for s in range(4)]
+        strip = keep.tile([P, 3 * T - 2 * LATE], F32, name="strip", align_bytes=64)
+        middle_gates = [keep.tile([P, T], F32, name="gate%d" % s, align_bytes=64) for s in (1, 2)]
+        outer_new = [keep.tile([P, T], F32, name="new%d" % s, align_bytes=64) for s in (0, 3)]
+        pairs = keep.tile([P, 2, U, 2], BF16, name="pairs", align_bytes=64)
         woven = [keep.tile([P, width, 2], I32, name="woven%d" % first, align_bytes=64) for first, width in PIECES]
         y_codes = keep.tile([P, U], U32, name="y_codes", align_bytes=64)
         y_plane = keep.tile([P, U], U8, name="y_plane", align_bytes=64)
         warm = keep.tile([P, 2], F32, name="warm")
 
-        lanes = (0, 1, 2, 3)
+        outer_gate = strip[:, T - LATE : 2 * T - LATE]
+        gate = [outer_gate, middle_gates[0][:], middle_gates[1][:], outer_gate]
+        new = [outer_new[0][:], strip[:, :T], strip[:, 2 * T - 2 * LATE :], outer_new[1][:]]
+
+        lanes = (0, 2, 3, 1)
         mem_rows = mem.rearrange("(p t) c -> p t c", t=PACK)
         out_rows = out_0.rearrange("(p t) c -> p t c", t=PACK)
         w_rows = w1.rearrange("(p j) c -> p j c", j=PACK)
@@ -88,51 +95,28 @@ def tile_picked_widxput_gate_lo_kernel(tc, x_words, x_scales, mem, w1, slot, out
         quantise_w(1)
         quantise_w(0)
 
-        def make_gate(s, first, width):
-            acc = psum.tile([P, width], F32, name="acc%d_%d" % (s, first))
+        def make_gate(s, first, last):
+            acc = psum.tile([P, last - first], F32, name="acc%d_%d" % (s, first))
             cols = slice(lanes[s] * P, (lanes[s] + 1) * P)
             nc.tensor.matmul_mx(out=acc[:], lhsT=w_codes[:, cols].bitcast(FP8X4), lhsT_scale=w_plane[:, cols],
-                                rhs=x_codes[:, first : first + width].bitcast(FP8X4),
-                                rhs_scale=x_plane[:, first : first + width], start=True, stop=True)
-            nc.scalar.activation(gate[s][:, first : first + width], acc[:], SIGMOID)
+                                rhs=x_codes[:, first:last].bitcast(FP8X4), rhs_scale=x_plane[:, first:last],
+                                start=True, stop=True)
+            nc.scalar.activation(gate[s][:, first:last], acc[:], SIGMOID)
 
-        make_gate(0, 0, HALF)
-        make_gate(0, HALF, HALF)
-        for s in range(1, 4):
-            make_gate(s, 0, T)
-
-        def entries(first, last):
-            return offsets[:, first // STRIPE : last // STRIPE]
+        def window(s, first, last):
+            return store[s][:].indirect(offsets[:, first // STRIPE : last // STRIPE])
 
         def look_up(s, first, last):
-            nc.vector.tensor_tensor(new[s][:, first:last], store[s][:].indirect(entries(first, last)), gate[s][:, first:last], MULT)
+            nc.vector.tensor_tensor(new[s][:, first:last], window(s, first, last), gate[s][:, first:last], MULT)
 
-        for first in (0, HALF):
-            cols = slice(first, first + HALF)
-            nc.vector.tensor_copy(old[:, cols], store[0][:].indirect(entries(first, first + HALF)))
-            nc.gpsimd.tensor_tensor(new[0][:, cols], old[:, cols], gate[0][:, cols], MULT)
-        nc.vector.tensor_copy(second_old[:, VECTOR_PUTS:], store[1][:].indirect(entries(VECTOR_PUTS, T)))
-        nc.gpsimd.tensor_tensor(new[1][:, VECTOR_PUTS:], second_old[:, VECTOR_PUTS:], gate[1][:, VECTOR_PUTS:], MULT)
-        nc.vector.tensor_copy(second_old[:, :VECTOR_PUTS], store[1][:].indirect(entries(0, VECTOR_PUTS)))
-        nc.vector.tensor_tensor(store[1][:].indirect(entries(0, VECTOR_PUTS)), second_old[:, :VECTOR_PUTS],
-                                gate[1][:, :VECTOR_PUTS], MULT)
-        look_up(2, 0, T)
-        look_up(3, 0, T)
-        nc.vector.tensor_copy(store[3][:].indirect(offsets[:]), new[3][:])
+        def scalar_put(s, first, last):
+            nc.scalar.activation(window(s, first, last), new[s][:, first:last], COPY)
 
-        def put(s, first, last):
-            nc.scalar.activation(store[s][:].indirect(entries(first, last)), new[s][:, first:last], COPY)
+        def vector_put(s, first, last):
+            nc.vector.tensor_copy(window(s, first, last), new[s][:, first:last])
 
-        put(0, 0, HALF)
-        put(0, HALF, T)
-        put(1, VECTOR_PUTS, T)
-        put(2, 0, HALF)
-        put(2, HALF, T)
-        for s in range(4):
+        def hand_out(s):
             nc.sync.dma_start(out_rows[:, lanes[s], :], store[s][:])
-
-        pairs = keep.tile([P, 2, U, 2], BF16, name="pairs", tag="gate3", align_bytes=64)
-        pair_words = pairs[:].rearrange("p u c e -> p u (c e)").bitcast(I32)
 
         def round_lane(copy, s, first, width):
             copy(pairs[:, lanes[s] // 2, first : first + width, lanes[s] % 2], store[s][:, first : first + width])
@@ -140,19 +124,49 @@ def tile_picked_widxput_gate_lo_kernel(tc, x_words, x_scales, mem, w1, slot, out
         def pool_copy(dst, src):
             nc.gpsimd.tensor_scalar(dst, src, 1.0, -0.0, MULT, ADD)
 
-        split, rest = PIECES[-1]
-        for s in (0, 1):
+        for first, last in zip(FIRST_CUTS, FIRST_CUTS[1:]):
+            make_gate(0, first, last)
+            look_up(0, first, last)
+        make_gate(1, 0, HALF)
+        make_gate(1, HALF, T)
+        look_up(1, 0, T - LATE)
+        make_gate(2, 0, HALF)
+        make_gate(2, HALF, T)
+        look_up(2, LATE, T)
+        scalar_put(0, 0, SHORT)
+        make_gate(3, 0, T)
+        scalar_put(0, SHORT, T)
+        hand_out(0)
+        look_up(3, 0, T)
+        look_up(1, T - LATE, T)
+        look_up(2, 0, LATE)
+        vector_put(3, 0, T)
+        hand_out(3)
+        scalar_put(1, 0, SHORT)
+        scalar_put(2, 0, SCALAR_PUTS)
+        scalar_put(1, SHORT, T)
+        vector_put(2, SCALAR_PUTS, T)
+        hand_out(2)
+        hand_out(1)
+
+        for s in (0, 3):
             round_lane(pool_copy, s, 0, U)
+        split, rest = PIECES[-1]
         round_lane(nc.vector.tensor_copy, 2, 0, split)
-        for s in (2, 3):
-            round_lane(nc.scalar.copy, s, split, rest)
+        runs = ((split, rest // 2), (split + rest // 2, rest // 2))
+        round_lane(nc.scalar.copy, 2, split, rest)
+        for first, width in runs:
+            round_lane(nc.scalar.copy, 1, first, width)
         for first, width in PIECES[:-1]:
-            round_lane(nc.vector.tensor_copy, 3, first, width)
+            round_lane(nc.vector.tensor_copy, 1, first, width)
+        pair_words = pairs[:].rearrange("p u c e -> p u (c e)").bitcast(I32)
         out_words = out_1[0].rearrange("p c r -> p (c r)").bitcast(I32)
         for tile, (first, width) in zip(woven, PIECES):
             src = pair_words[:, :, first : first + width].rearrange("p u c -> p c u")
             if first == split:
-                nc.scalar.copy(tile[:].bitcast(U32), src.bitcast(U32))
+                for at, size in runs:
+                    part = slice(at - split, at - split + size)
+                    nc.scalar.copy(tile[:, part].bitcast(U32), src[:, part].bitcast(U32))
             else:
                 nc.vector.tensor_copy(tile[:], src)
         for tile, (first, width) in zip(woven, PIECES):

@@ -20,10 +20,7 @@ STRIPE = 16
 QUADRANTS = 4
 K, T, N, U = 512, 512, 512, 1024
 HALF = 256
-GROUPS = HALF // PACK
 PIECES = ((0, 256), (256, 384), (640, 384))
-W_FIRST = 384
-W_SCALAR = 10
 FIRST_CUTS = (0, 128, 256, 512)
 LATE = 64
 SHORT = 128
@@ -40,8 +37,8 @@ def tile_picked_widxput_gate_lo_kernel(tc, x_words, x_scales, mem, w1, slot, out
         offsets = keep.tile([P, T // STRIPE], U16, name="offsets")
         x_codes = keep.tile([P, T], U32, name="x_codes", align_bytes=64)
         x_plane = keep.tile([P, T], U8, name="x_plane", align_bytes=64)
-        w_raw = [keep.tile([P, PACK, width], F32, name="w_raw%d" % width, align_bytes=64) for width in (W_FIRST, N - W_FIRST)]
-        w_dealt = [keep.tile([P, PACK, GROUPS, PACK], BF16, name="w_dealt%d" % h, align_bytes=64) for h in range(2)]
+        w_raw = [keep.tile([P, 2, N], F32, name="w_raw%d" % h, align_bytes=64) for h in range(2)]
+        w_dealt = keep.tile([P, PACK, P, PACK], BF16, name="w_dealt", align_bytes=64)
         w_codes = keep.tile([P, N], U32, name="w_codes", align_bytes=64)
         w_plane = keep.tile([P, N], U8, name="w_plane", align_bytes=64)
         store = [keep.tile([P, U], F32, name="store%d" % s, align_bytes=64) for s in range(4)]
@@ -68,32 +65,26 @@ def tile_picked_widxput_gate_lo_kernel(tc, x_words, x_scales, mem, w1, slot, out
         nc.scalar.activation(warm[:, 1:2], warm[:, 0:1], SIGMOID)
 
         nc.sync.dma_start(offsets[:], slot)
-        nc.sync.dma_start(w_raw[0][:], w_rows[:, :, :W_FIRST])
-        nc.sync.dma_start(w_raw[1][:], w_rows[:, :, W_FIRST:])
+        for h in range(2):
+            nc.sync.dma_start(w_raw[h][:], w_rows[:, 2 * h : 2 * h + 2, :])
         for q in range(QUADRANTS):
             nc.sync.dma_start(x_plane[32 * q : 32 * q + 4, :].bitcast(I32), x_scales[0][4 * q : 4 * q + 4, :].bitcast(I32))
         nc.sync.dma_start(x_codes[:].bitcast(I32), x_words[0].rearrange("p c r -> p (c r)").bitcast(I32))
         for s in range(4):
             nc.sync.dma_start(store[s][:], mem_rows[:, lanes[s], :])
 
-        def round_w(copy, first, last):
-            h, at = divmod(first, GROUPS)
-            raw, start = (w_raw[0], first) if first < W_FIRST // PACK else (w_raw[1], first - W_FIRST // PACK)
-            copy(w_dealt[h][:, :, at : at + last - first, :].rearrange("p t g j -> p g t j"),
-                 raw[:].rearrange("p j (g t) -> p g t j", t=PACK)[:, start : start + last - first])
+        def round_w(copy, h, first, last, step=1):
+            copy(w_dealt[:, first:last:step, :, 2 * h : 2 * h + 2].rearrange("p t (g i) j -> p g t i j", i=2),
+                 w_raw[h][:].rearrange("p j (g i t) -> p g t i j", i=2, t=PACK)[:, :, first:last:step])
 
-        def quantise_w(h):
-            for s in range(4):
-                at = lanes[s] * P + h * GROUPS
-                nc.vector.quantize_mx(out=w_codes[:, at : at + GROUPS].bitcast(FP8X4), scales=w_plane[:, at : at + GROUPS],
-                                      in_=w_dealt[h][:, lanes[s]].rearrange("p g j -> p (g j)"))
-
-        round_w(nc.vector.tensor_copy, 0, GROUPS)
-        round_w(nc.scalar.copy, GROUPS, W_FIRST // PACK)
-        round_w(nc.vector.tensor_copy, W_FIRST // PACK, P - W_SCALAR)
-        round_w(nc.scalar.copy, P - W_SCALAR, P)
-        quantise_w(1)
-        quantise_w(0)
+        round_w(nc.vector.tensor_copy, 0, 0, PACK)
+        round_w(nc.vector.tensor_copy, 1, 0, 1)
+        round_w(nc.vector.tensor_copy, 1, 2, 3)
+        round_w(nc.scalar.copy, 1, 1, PACK, 2)
+        for s in range(4):
+            cols = slice(lanes[s] * P, (lanes[s] + 1) * P)
+            nc.vector.quantize_mx(out=w_codes[:, cols].bitcast(FP8X4), scales=w_plane[:, cols],
+                                  in_=w_dealt[:, lanes[s]].rearrange("p g j -> p (g j)"))
 
         def make_gate(s, first, last):
             acc = psum.tile([P, last - first], F32, name="acc%d_%d" % (s, first))

@@ -24,7 +24,7 @@ PIECES = ((0, 256), (256, 384), (640, 384))
 FIRST_CUTS = (0, 128, 256, 512)
 LATE = 64
 SHORT = 128
-SCALAR_PUTS = 288
+SCALAR_PUTS = 256
 FLOPS = 2 * K * N * T
 
 
@@ -64,12 +64,12 @@ def tile_picked_widxput_gate_lo_kernel(tc, x_words, x_scales, mem, w1, slot, out
         nc.vector.memset(warm[:, 0:1], 0.0)
         nc.scalar.activation(warm[:, 1:2], warm[:, 0:1], SIGMOID)
 
-        nc.sync.dma_start(offsets[:], slot)
         for h in range(2):
             nc.sync.dma_start(w_raw[h][:], w_rows[:, 2 * h : 2 * h + 2, :])
         for q in range(QUADRANTS):
             nc.sync.dma_start(x_plane[32 * q : 32 * q + 4, :].bitcast(I32), x_scales[0][4 * q : 4 * q + 4, :].bitcast(I32))
         nc.sync.dma_start(x_codes[:].bitcast(I32), x_words[0].rearrange("p c r -> p (c r)").bitcast(I32))
+        nc.sync.dma_start(offsets[:], slot)
         for s in range(4):
             nc.sync.dma_start(store[s][:], mem_rows[:, lanes[s], :])
 

@@ -24,7 +24,7 @@ PIECES = ((0, 256), (256, 384), (640, 384))
 FIRST_CUTS = (0, 128, 256, 512)
 LATE = 64
 SHORT = 128
-SCALAR_PUTS = 256
+SCALAR_PUTS = 224
 FLOPS = 2 * K * N * T
 
 
@@ -128,7 +128,8 @@ def tile_picked_widxput_gate_lo_kernel(tc, x_words, x_scales, mem, w1, slot, out
         make_gate(3, 0, T)
         scalar_put(0, SHORT, T)
         hand_out(0)
-        look_up(3, 0, T)
+        for first, last in ((0, SHORT), (T - SHORT, T), (SHORT, T - SHORT)):
+            look_up(3, first, last)
         look_up(1, T - LATE, T)
         look_up(2, 0, LATE)
         vector_put(3, 0, T)

@@ -20,7 +20,8 @@ STRIPE = 16
 QUADRANTS = 4
 K, T, N, U = 512, 512, 512, 1024
 HALF = 256
-PIECES = ((0, 256), (256, 384), (640, 384))
+PIECES = ((0, 256), (256, 640), (640, 1024))
+VECTOR_COLUMNS = 672
 FIRST_CUTS = (0, 128, 256, 512)
 LATE = 64
 SHORT = 128
@@ -46,7 +47,7 @@ def tile_picked_widxput_gate_lo_kernel(tc, x_words, x_scales, mem, w1, slot, out
         middle_gates = [keep.tile([P, T], F32, name="gate%d" % s, align_bytes=64) for s in (1, 2)]
         outer_new = [keep.tile([P, T], F32, name="new%d" % s, align_bytes=64) for s in (0, 3)]
         pairs = keep.tile([P, 2, U, 2], BF16, name="pairs", align_bytes=64)
-        woven = [keep.tile([P, width, 2], I32, name="woven%d" % first, align_bytes=64) for first, width in PIECES]
+        woven = keep.tile([P, 2 * U], I32, name="woven", align_bytes=64)
         y_codes = keep.tile([P, U], U32, name="y_codes", align_bytes=64)
         y_plane = keep.tile([P, U], U8, name="y_plane", align_bytes=64)
         warm = keep.tile([P, 2], F32, name="warm")
@@ -143,28 +144,22 @@ def tile_picked_widxput_gate_lo_kernel(tc, x_words, x_scales, mem, w1, slot, out
 
         for s in (0, 3):
             round_lane(pool_copy, s, 0, U)
-        split, rest = PIECES[-1]
-        round_lane(nc.vector.tensor_copy, 2, 0, split)
-        runs = ((split, rest // 2), (split + rest // 2, rest // 2))
-        round_lane(nc.scalar.copy, 2, split, rest)
-        for first, width in runs:
-            round_lane(nc.scalar.copy, 1, first, width)
-        for first, width in PIECES[:-1]:
-            round_lane(nc.vector.tensor_copy, 1, first, width)
-        pair_words = pairs[:].rearrange("p u c e -> p u (c e)").bitcast(I32)
+        middle = (VECTOR_COLUMNS + U) // 2
+        vector_runs = ((0, 256), (256, VECTOR_COLUMNS))
+        scalar_runs = ((VECTOR_COLUMNS, middle), (middle, U))
+        round_lane(nc.vector.tensor_copy, 2, 0, VECTOR_COLUMNS)
+        round_lane(nc.scalar.copy, 2, VECTOR_COLUMNS, U - VECTOR_COLUMNS)
+        pair_words = pairs[:].rearrange("p u c e -> p u (c e)")
+        for copy, word, runs in ((nc.vector.tensor_copy, I32, vector_runs), (nc.scalar.copy, U32, scalar_runs)):
+            for first, last in runs:
+                round_lane(copy, 1, first, last - first)
+            for first, last in runs:
+                copy(woven[:, 2 * first : 2 * last].bitcast(word).rearrange("p (c u) -> p c u", u=2),
+                     pair_words.bitcast(word)[:, :, first:last].rearrange("p u c -> p c u"))
         out_words = out_1[0].rearrange("p c r -> p (c r)").bitcast(I32)
-        for tile, (first, width) in zip(woven, PIECES):
-            src = pair_words[:, :, first : first + width].rearrange("p u c -> p c u")
-            if first == split:
-                for at, size in runs:
-                    part = slice(at - split, at - split + size)
-                    nc.scalar.copy(tile[:, part].bitcast(U32), src[:, part].bitcast(U32))
-            else:
-                nc.vector.tensor_copy(tile[:], src)
-        for tile, (first, width) in zip(woven, PIECES):
-            cols = slice(first, first + width)
-            nc.vector.quantize_mx(out=y_codes[:, cols].bitcast(FP8X4), scales=y_plane[:, cols],
-                                  in_=tile[:].rearrange("p c u -> p (c u)").bitcast(BF16))
-            nc.sync.dma_start(out_words[:, cols], y_codes[:, cols].bitcast(I32))
+        for first, last in PIECES:
+            nc.vector.quantize_mx(out=y_codes[:, first:last].bitcast(FP8X4), scales=y_plane[:, first:last],
+                                  in_=woven[:, 2 * first : 2 * last].bitcast(BF16))
+            nc.sync.dma_start(out_words[:, first:last], y_codes[:, first:last].bitcast(I32))
         for q in range(QUADRANTS):
             nc.sync.dma_start(out_2[0][4 * q : 4 * q + 4, :].bitcast(I32), y_plane[32 * q : 32 * q + 4, :].bitcast(I32))

@@ -19,13 +19,15 @@ PACK = 4
 STRIPE = 16
 QUADRANTS = 4
 K, T, N, U = 512, 512, 512, 1024
-HALF = 256
-PIECES = ((0, 256), (256, 640), (640, 1024))
-VECTOR_COLUMNS = 672
+LANES = (0, 2, 3, 1)
+HALF = T // 2
 FIRST_CUTS = (0, 128, 256, 512)
 LATE = 64
 SHORT = 128
 SCALAR_PUTS = 224
+VECTOR_COLUMNS = 664
+QUANTISE_CUTS = (0, 256, 640, 768, 1024)
+STORE_CUTS = (0, 256, 640, 1024)
 FLOPS = 2 * K * N * T
 
 
@@ -42,7 +44,7 @@ def tile_picked_widxput_gate_lo_kernel(tc, x_words, x_scales, mem, w1, slot, out
         w_dealt = keep.tile([P, PACK, P, PACK], BF16, name="w_dealt", align_bytes=64)
         w_codes = keep.tile([P, N], U32, name="w_codes", align_bytes=64)
         w_plane = keep.tile([P, N], U8, name="w_plane", align_bytes=64)
-        store = [keep.tile([P, U], F32, name="store%d" % s, align_bytes=64) for s in range(4)]
+        store = [keep.tile([P, U], F32, name="store%d" % s, align_bytes=64) for s in range(PACK)]
         strip = keep.tile([P, 3 * T - 2 * LATE], F32, name="strip", align_bytes=64)
         middle_gates = [keep.tile([P, T], F32, name="gate%d" % s, align_bytes=64) for s in (1, 2)]
         outer_new = [keep.tile([P, T], F32, name="new%d" % s, align_bytes=64) for s in (0, 3)]
@@ -56,7 +58,6 @@ def tile_picked_widxput_gate_lo_kernel(tc, x_words, x_scales, mem, w1, slot, out
         gate = [outer_gate, middle_gates[0][:], middle_gates[1][:], outer_gate]
         new = [outer_new[0][:], strip[:, :T], strip[:, 2 * T - 2 * LATE :], outer_new[1][:]]
 
-        lanes = (0, 2, 3, 1)
         mem_rows = mem.rearrange("(p t) c -> p t c", t=PACK)
         out_rows = out_0.rearrange("(p t) c -> p t c", t=PACK)
         w_rows = w1.rearrange("(p j) c -> p j c", j=PACK)
@@ -71,25 +72,25 @@ def tile_picked_widxput_gate_lo_kernel(tc, x_words, x_scales, mem, w1, slot, out
             nc.sync.dma_start(x_plane[32 * q : 32 * q + 4, :].bitcast(I32), x_scales[0][4 * q : 4 * q + 4, :].bitcast(I32))
         nc.sync.dma_start(x_codes[:].bitcast(I32), x_words[0].rearrange("p c r -> p (c r)").bitcast(I32))
         nc.sync.dma_start(offsets[:], slot)
-        for s in range(4):
-            nc.sync.dma_start(store[s][:], mem_rows[:, lanes[s], :])
+        for s in range(PACK):
+            nc.sync.dma_start(store[s][:], mem_rows[:, LANES[s], :])
 
-        def round_w(copy, h, first, last, step=1):
-            copy(w_dealt[:, first:last:step, :, 2 * h : 2 * h + 2].rearrange("p t (g i) j -> p g t i j", i=2),
-                 w_raw[h][:].rearrange("p j (g i t) -> p g t i j", i=2, t=PACK)[:, :, first:last:step])
+        def round_w(copy, h, lanes):
+            copy(w_dealt[:, lanes, :, 2 * h : 2 * h + 2].rearrange("p t (g i) j -> p g t i j", i=2),
+                 w_raw[h][:].rearrange("p j (g i t) -> p g t i j", i=2, t=PACK)[:, :, lanes])
 
-        round_w(nc.vector.tensor_copy, 0, 0, PACK)
-        round_w(nc.vector.tensor_copy, 1, 0, 1)
-        round_w(nc.vector.tensor_copy, 1, 2, 3)
-        round_w(nc.scalar.copy, 1, 1, PACK, 2)
-        for s in range(4):
-            cols = slice(lanes[s] * P, (lanes[s] + 1) * P)
+        round_w(nc.vector.tensor_copy, 0, slice(0, PACK))
+        for s in (0, 1):
+            round_w(nc.vector.tensor_copy, 1, slice(LANES[s], LANES[s] + 1))
+        round_w(nc.scalar.copy, 1, slice(1, PACK, 2))
+        for lane in LANES:
+            cols = slice(lane * P, (lane + 1) * P)
             nc.vector.quantize_mx(out=w_codes[:, cols].bitcast(FP8X4), scales=w_plane[:, cols],
-                                  in_=w_dealt[:, lanes[s]].rearrange("p g j -> p (g j)"))
+                                  in_=w_dealt[:, lane].rearrange("p m j -> p (m j)"))
 
         def make_gate(s, first, last):
             acc = psum.tile([P, last - first], F32, name="acc%d_%d" % (s, first))
-            cols = slice(lanes[s] * P, (lanes[s] + 1) * P)
+            cols = slice(LANES[s] * P, (LANES[s] + 1) * P)
             nc.tensor.matmul_mx(out=acc[:], lhsT=w_codes[:, cols].bitcast(FP8X4), lhsT_scale=w_plane[:, cols],
                                 rhs=x_codes[:, first:last].bitcast(FP8X4), rhs_scale=x_plane[:, first:last],
                                 start=True, stop=True)
@@ -108,10 +109,10 @@ def tile_picked_widxput_gate_lo_kernel(tc, x_words, x_scales, mem, w1, slot, out
             nc.vector.tensor_copy(window(s, first, last), new[s][:, first:last])
 
         def hand_out(s):
-            nc.sync.dma_start(out_rows[:, lanes[s], :], store[s][:])
+            nc.sync.dma_start(out_rows[:, LANES[s], :], store[s][:])
 
-        def round_lane(copy, s, first, width):
-            copy(pairs[:, lanes[s] // 2, first : first + width, lanes[s] % 2], store[s][:, first : first + width])
+        def round_lane(copy, s, first, last):
+            copy(pairs[:, LANES[s] // 2, first:last, LANES[s] % 2], store[s][:, first:last])
 
         def pool_copy(dst, src):
             nc.gpsimd.tensor_scalar(dst, src, 1.0, -0.0, MULT, ADD)
@@ -144,22 +145,22 @@ def tile_picked_widxput_gate_lo_kernel(tc, x_words, x_scales, mem, w1, slot, out
 
         for s in (0, 3):
             round_lane(pool_copy, s, 0, U)
-        middle = (VECTOR_COLUMNS + U) // 2
-        vector_runs = ((0, 256), (256, VECTOR_COLUMNS))
-        scalar_runs = ((VECTOR_COLUMNS, middle), (middle, U))
+        vector_runs = ((0, QUANTISE_CUTS[1]), (QUANTISE_CUTS[1], VECTOR_COLUMNS))
+        scalar_runs = ((VECTOR_COLUMNS, QUANTISE_CUTS[-2]), (QUANTISE_CUTS[-2], U))
         round_lane(nc.vector.tensor_copy, 2, 0, VECTOR_COLUMNS)
-        round_lane(nc.scalar.copy, 2, VECTOR_COLUMNS, U - VECTOR_COLUMNS)
+        round_lane(nc.scalar.copy, 2, VECTOR_COLUMNS, U)
         pair_words = pairs[:].rearrange("p u c e -> p u (c e)")
         for copy, word, runs in ((nc.vector.tensor_copy, I32, vector_runs), (nc.scalar.copy, U32, scalar_runs)):
             for first, last in runs:
-                round_lane(copy, 1, first, last - first)
+                round_lane(copy, 1, first, last)
             for first, last in runs:
                 copy(woven[:, 2 * first : 2 * last].bitcast(word).rearrange("p (c u) -> p c u", u=2),
                      pair_words.bitcast(word)[:, :, first:last].rearrange("p u c -> p c u"))
         out_words = out_1[0].rearrange("p c r -> p (c r)").bitcast(I32)
-        for first, last in PIECES:
+        for first, last in zip(QUANTISE_CUTS, QUANTISE_CUTS[1:]):
             nc.vector.quantize_mx(out=y_codes[:, first:last].bitcast(FP8X4), scales=y_plane[:, first:last],
                                   in_=woven[:, 2 * first : 2 * last].bitcast(BF16))
+        for first, last in zip(STORE_CUTS, STORE_CUTS[1:]):
             nc.sync.dma_start(out_words[:, first:last], y_codes[:, first:last].bitcast(I32))
         for q in range(QUADRANTS):
             nc.sync.dma_start(out_2[0][4 * q : 4 * q + 4, :].bitcast(I32), y_plane[32 * q : 32 * q + 4, :].bitcast(I32))

from contextlib import ExitStack

import concourse.mybir as mybir

F32 = mybir.dt.float32
BF16 = mybir.dt.bfloat16
I32 = mybir.dt.int32
U32 = mybir.dt.uint32
U16 = mybir.dt.uint16
U8 = mybir.dt.uint8
FP8X4 = mybir.dt.float8_e4m3fn_x4
SIGMOID = mybir.ActivationFunctionType.Sigmoid
COPY = mybir.ActivationFunctionType.Copy
MULT = mybir.AluOpType.mult
ADD = mybir.AluOpType.add

P = 128
PACK = 4
STRIPE = 16
QUADRANTS = 4
K, T, N, U = 512, 512, 512, 1024
LANES = (0, 2, 3, 1)
HALF = T // 2
FIRST_CUTS = (0, 128, 256, 512)
LATE = 64
SHORT = 128
SCALAR_PUTS = 224
VECTOR_COLUMNS = 664
QUANTISE_CUTS = (0, 256, 640, 768, 1024)
STORE_CUTS = (0, 256, 640, 1024)
FLOPS = 2 * K * N * T


def tile_picked_widxput_gate_lo_kernel(tc, x_words, x_scales, mem, w1, slot, out_0, out_1, out_2):
    nc = tc.nc
    with ExitStack() as ctx:
        keep = ctx.enter_context(tc.tile_pool(name="keep", bufs=1))
        psum = ctx.enter_context(tc.psum_pool(name="psum", bufs=1))

        offsets = keep.tile([P, T // STRIPE], U16, name="offsets")
        x_codes = keep.tile([P, T], U32, name="x_codes", align_bytes=64)
        x_plane = keep.tile([P, T], U8, name="x_plane", align_bytes=64)
        w_raw = [keep.tile([P, 2, N], F32, name="w_raw%d" % h, align_bytes=64) for h in range(2)]
        w_dealt = keep.tile([P, PACK, P, PACK], BF16, name="w_dealt", align_bytes=64)
        w_codes = keep.tile([P, N], U32, name="w_codes", align_bytes=64)
        w_plane = keep.tile([P, N], U8, name="w_plane", align_bytes=64)
        store = [keep.tile([P, U], F32, name="store%d" % s, align_bytes=64) for s in range(PACK)]
        strip = keep.tile([P, 3 * T - 2 * LATE], F32, name="strip", align_bytes=64)
        middle_gates = [keep.tile([P, T], F32, name="gate%d" % s, align_bytes=64) for s in (1, 2)]
        outer_new = [keep.tile([P, T], F32, name="new%d" % s, align_bytes=64) for s in (0, 3)]
        pairs = keep.tile([P, 2, U, 2], BF16, name="pairs", align_bytes=64)
        woven = keep.tile([P, 2 * U], I32, name="woven", align_bytes=64)
        y_codes = keep.tile([P, U], U32, name="y_codes", align_bytes=64)
        y_plane = keep.tile([P, U], U8, name="y_plane", align_bytes=64)
        warm = keep.tile([P, 2], F32, name="warm")

        outer_gate = strip[:, T - LATE : 2 * T - LATE]
        gate = [outer_gate, middle_gates[0][:], middle_gates[1][:], outer_gate]
        new = [outer_new[0][:], strip[:, :T], strip[:, 2 * T - 2 * LATE :], outer_new[1][:]]

        mem_rows = mem.rearrange("(p t) c -> p t c", t=PACK)
        out_rows = out_0.rearrange("(p t) c -> p t c", t=PACK)
        w_rows = w1.rearrange("(p j) c -> p j c", j=PACK)

        nc.vector.memset(x_plane[:].bitcast(I32), 0)
        nc.vector.memset(warm[:, 0:1], 0.0)
        nc.scalar.activation(warm[:, 1:2], warm[:, 0:1], SIGMOID)

        for h in range(2):
            nc.sync.dma_start(w_raw[h][:], w_rows[:, 2 * h : 2 * h + 2, :])
        for q in range(QUADRANTS):
            nc.sync.dma_start(x_plane[32 * q : 32 * q + 4, :].bitcast(I32), x_scales[0][4 * q : 4 * q + 4, :].bitcast(I32))
        nc.sync.dma_start(x_codes[:].bitcast(I32), x_words[0].rearrange("p c r -> p (c r)").bitcast(I32))
        nc.sync.dma_start(offsets[:], slot)
        for s in range(PACK):
            nc.sync.dma_start(store[s][:], mem_rows[:, LANES[s], :])

        def round_w(copy, h, lanes):
            copy(w_dealt[:, lanes, :, 2 * h : 2 * h + 2].rearrange("p t (g i) j -> p g t i j", i=2),
                 w_raw[h][:].rearrange("p j (g i t) -> p g t i j", i=2, t=PACK)[:, :, lanes])

        round_w(nc.vector.tensor_copy, 0, slice(0, PACK))
        for s in (0, 1):
            round_w(nc.vector.tensor_copy, 1, slice(LANES[s], LANES[s] + 1))
        round_w(nc.scalar.copy, 1, slice(1, PACK, 2))
        for lane in LANES:
            cols = slice(lane * P, (lane + 1) * P)
            nc.vector.quantize_mx(out=w_codes[:, cols].bitcast(FP8X4), scales=w_plane[:, cols],
                                  in_=w_dealt[:, lane].rearrange("p m j -> p (m j)"))

        def make_gate(s, first, last):
            acc = psum.tile([P, last - first], F32, name="acc%d_%d" % (s, first))
            cols = slice(LANES[s] * P, (LANES[s] + 1) * P)
            nc.tensor.matmul_mx(out=acc[:], lhsT=w_codes[:, cols].bitcast(FP8X4), lhsT_scale=w_plane[:, cols],
                                rhs=x_codes[:, first:last].bitcast(FP8X4), rhs_scale=x_plane[:, first:last],
                                start=True, stop=True)
            nc.scalar.activation(gate[s][:, first:last], acc[:], SIGMOID)

        def window(s, first, last):
            return store[s][:].indirect(offsets[:, first // STRIPE : last // STRIPE])

        def look_up(s, first, last):
            nc.vector.tensor_tensor(new[s][:, first:last], window(s, first, last), gate[s][:, first:last], MULT)

        def scalar_put(s, first, last):
            nc.scalar.activation(window(s, first, last), new[s][:, first:last], COPY)

        def vector_put(s, first, last):
            nc.vector.tensor_copy(window(s, first, last), new[s][:, first:last])

        def hand_out(s):
            nc.sync.dma_start(out_rows[:, LANES[s], :], store[s][:])

        def round_lane(copy, s, first, last):
            copy(pairs[:, LANES[s] // 2, first:last, LANES[s] % 2], store[s][:, first:last])

        def pool_copy(dst, src):
            nc.gpsimd.tensor_scalar(dst, src, 1.0, -0.0, MULT, ADD)

        for first, last in zip(FIRST_CUTS, FIRST_CUTS[1:]):
            make_gate(0, first, last)
            look_up(0, first, last)
        make_gate(1, 0, HALF)
        make_gate(1, HALF, T)
        look_up(1, 0, T - LATE)
        make_gate(2, 0, HALF)
        make_gate(2, HALF, T)
        look_up(2, LATE, T)
        scalar_put(0, 0, SHORT)
        make_gate(3, 0, T)
        scalar_put(0, SHORT, T)
        hand_out(0)
        for first, last in ((0, SHORT), (T - SHORT, T), (SHORT, T - SHORT)):
            look_up(3, first, last)
        look_up(1, T - LATE, T)
        look_up(2, 0, LATE)
        vector_put(3, 0, T)
        hand_out(3)
        scalar_put(1, 0, SHORT)
        scalar_put(2, 0, SCALAR_PUTS)
        scalar_put(1, SHORT, T)
        vector_put(2, SCALAR_PUTS, T)
        hand_out(2)
        hand_out(1)

        for s in (0, 3):
            round_lane(pool_copy, s, 0, U)
        vector_runs = ((0, QUANTISE_CUTS[1]), (QUANTISE_CUTS[1], VECTOR_COLUMNS))
        scalar_runs = ((VECTOR_COLUMNS, QUANTISE_CUTS[-2]), (QUANTISE_CUTS[-2], U))
        round_lane(nc.vector.tensor_copy, 2, 0, VECTOR_COLUMNS)
        round_lane(nc.scalar.copy, 2, VECTOR_COLUMNS, U)
        pair_words = pairs[:].rearrange("p u c e -> p u (c e)")
        for copy, word, runs in ((nc.vector.tensor_copy, I32, vector_runs), (nc.scalar.copy, U32, scalar_runs)):
            for first, last in runs:
                round_lane(copy, 1, first, last)
            for first, last in runs:
                copy(woven[:, 2 * first : 2 * last].bitcast(word).rearrange("p (c u) -> p c u", u=2),
                     pair_words.bitcast(word)[:, :, first:last].rearrange("p u c -> p c u"))
        out_words = out_1[0].rearrange("p c r -> p (c r)").bitcast(I32)
        for first, last in zip(QUANTISE_CUTS, QUANTISE_CUTS[1:]):
            nc.vector.quantize_mx(out=y_codes[:, first:last].bitcast(FP8X4), scales=y_plane[:, first:last],
                                  in_=woven[:, 2 * first : 2 * last].bitcast(BF16))
        for first, last in zip(STORE_CUTS, STORE_CUTS[1:]):
            nc.sync.dma_start(out_words[:, first:last], y_codes[:, first:last].bitcast(I32))
        for q in range(QUADRANTS):
            nc.sync.dma_start(out_2[0][4 * q : 4 * q + 4, :].bitcast(I32), y_plane[32 * q : 32 * q + 4, :].bitcast(I32))
